import numpy as np
import ml_dtypes


def mxq(x, axis, fmt="e4m3"):
    dtype, down = {"e4m3": (ml_dtypes.float8_e4m3fn, 7), "e5m2": (ml_dtypes.float8_e5m2, 14)}[fmt]
    v = np.moveaxis(np.asarray(x, np.float32).astype(ml_dtypes.bfloat16).astype(np.float64), axis, -1)
    blocks = v.reshape(v.shape[:-1] + (-1, 32))
    amax = np.abs(blocks).max(-1, keepdims=True)
    byte = np.maximum(np.where(amax > 0, np.frexp(amax)[1] - 1 + 127, 0) - down, 1)
    scale = np.exp2(byte - 127.0)
    codes = (blocks / scale).astype(np.float32).astype(dtype).astype(np.float64)
    return np.moveaxis((codes * scale).reshape(v.shape), -1, axis)


WIDE = False


def mx_kscale(k):
    if not WIDE:
        return np.ones(k)
    levels = np.array([10, -10, 5, -5, 0])
    if k % 512:
        return np.exp2(np.random.permutation(np.resize(levels, k // 32))).repeat(32)
    a = np.empty((k // 512, 16))
    for p in range(k // 512):
        a[p, :8] = np.random.permutation(np.resize(levels, 8))
        for g in range(8):
            far = levels[np.abs(levels - a[p, g]) >= 10]
            a[p, g + 8] = far[np.random.randint(len(far))]
    return np.exp2(a.ravel()).repeat(32)


def f64(x):
    return np.asarray(x).astype(np.float64)


def striped(idx):
    return np.tile(idx.reshape(-1, 16).T, (8, 1)).astype(np.uint16)


def unstriped(offs):
    return offs[:16].T.reshape(-1).astype(np.int64)


E2M1 = np.array([0.0, 0.5, 1.0, 1.5, 2.0, 3.0, 4.0, 6.0, -0.0, -0.5, -1.0, -1.5, -2.0, -3.0, -4.0, -6.0])


def pack_weight(w, fmt):
    k, n = w.shape
    w = f64(np.asarray(w, np.float32).astype(ml_dtypes.bfloat16)).reshape(k // 32, 32, n)
    amax = np.abs(w).max(1)
    if fmt == "e4m3":
        byte = np.frexp(amax)[1] - 1 + 127 - 7
    else:
        mant, ex = np.frexp(amax / 6.0)
        byte = np.where(mant > 0.5, ex, ex - 1) + 127
    byte = np.clip(np.where(amax > 0, byte, 1), 1, 254)
    scaled = (w * np.exp2(127.0 - byte)[:, None, :]).reshape(k, n).astype(np.float32)
    by_word = np.ascontiguousarray(scaled.reshape(k // 512, 128, 4, n).transpose(0, 1, 3, 2))
    if fmt == "e4m3":
        words = by_word.astype(ml_dtypes.float8_e4m3fn).view(np.uint8)
    else:
        c = by_word.astype(ml_dtypes.float4_e2m1fn).view(np.uint8) & 0xF
        words = (c[..., 0::2] | (c[..., 1::2] << 4)).reshape(k // 512, 128, 2 * n)
    return np.ascontiguousarray(words), np.ascontiguousarray(byte.astype(np.uint8).reshape(k // 512, 16, n))


def unpack_weight(words, scales, fmt):
    g, _, n = scales.shape
    words = np.ascontiguousarray(words).reshape(g, 128, n, -1)
    if fmt == "e4m3":
        vals = words.view(ml_dtypes.float8_e4m3fn).astype(np.float64)
    else:
        nib = np.empty((g, 128, n, 4), np.uint8)
        nib[..., 0::2] = words & 0xF
        nib[..., 1::2] = words >> 4
        vals = E2M1[nib]
    vals = vals * np.repeat(np.exp2(scales.astype(np.float64) - 127.0), 8, axis=1)[..., None]
    return vals.transpose(0, 1, 3, 2).reshape(g * 512, n)


def gelu(v):
    return 0.5 * v * (1.0 + np.tanh(np.sqrt(2.0 / np.pi) * (v + 0.044715 * v**3)))


K, T, E, C, H, N = 512, 1024, 16, 128, 512, 256


def by_expert(wq, xq):
    return np.concatenate([wq[e].T @ xq[:, e * C:(e + 1) * C] for e in range(E)], axis=1)


def setup_inputs():
    n = np.random.standard_normal
    s = mx_kscale(K)
    u = mx_kscale(H)
    first = np.random.permutation(np.repeat(np.arange(E), T // E))
    second = (first + 1 + np.random.permutation(np.repeat(np.arange(E - 1), -(-T // (E - 1)))[:T])) % E
    while np.bincount(second, minlength=E).max() != T // E:
        load = np.bincount(second, minlength=E); hi, lo = int(load.argmax()), int(load.argmin())
        t = np.flatnonzero((second == hi) & (first != lo))[0]; second[t] = lo
    slot_token = np.empty(E * C, np.int64); pos = np.empty((2, T), np.int64); fill = np.zeros(E, np.int64)
    place = np.stack([np.random.permutation(C) for _ in range(E)])
    for r, deal in enumerate((first, second)):
        for t in np.random.permutation(T):
            e = deal[t]; j = e * C + place[e, fill[e]]; fill[e] += 1; slot_token[j] = t; pos[r, t] = j
    g = np.random.uniform(0.2, 0.8, T)
    x = pack_weight(n((K, T)) * s[:, None], "e4m3")
    return {
        "x_words": x[0],
        "x_scales": x[1],
        "w1": (n((K, H)) / np.sqrt(K) / s[:, None] * u).astype(np.float32),
        "w2": (n((E, H, N)) / np.sqrt(H) / u[None, :, None]).astype(np.float32),
        "gate": np.stack([np.tile(g, (128, 1)), np.tile(1.0 - g, (128, 1))]).astype(np.float32),
        "offs": striped(slot_token),
        "pos1": striped(pos[0]),
        "pos2": striped(pos[1]),
    }


def reference(x_words, x_scales, w1, w2, gate, offs, pos1, pos2):
    w1q = mxq(f64(w1), 0, "e4m3")
    w2q = mxq(f64(w2), 1, "e4m3")
    idx = unstriped(offs)
    x = unpack_weight(x_words, x_scales, "e4m3")
    h = gelu(w1q.T @ x)
    y = by_expert(w2q, mxq(h[:, idx], 0, "e4m3"))
    out = sum(f64(gate[r, :1]) * y[:, unstriped(p)] for r, p in enumerate((pos1, pos2)))
    return out

@@ -1,0 +1,285 @@
+from contextlib import ExitStack
+
+import concourse.mybir as mybir
+
+K, T, E, C, H, N = 512, 1024, 16, 128, 512, 256
+S = E * C
+FLOPS = 2 * K * H * T + 2 * H * N * S
+
+F32 = mybir.dt.float32
+BF16 = mybir.dt.bfloat16
+I32 = mybir.dt.int32
+U32 = mybir.dt.uint32
+U16 = mybir.dt.uint16
+U8 = mybir.dt.uint8
+FP8X4 = mybir.dt.float8_e4m3fn_x4
+MULT = mybir.AluOpType.mult
+ADD = mybir.AluOpType.add
+GELU = mybir.ActivationFunctionType.Gelu_apprx_tanh
+
+P = 128
+TOK = 256
+GROUP = 4
+GS = GROUP * C
+SPLIT = 14
+LATE = 11
+PIECES = ((512, 512), (512, 256, 256))
+
+
+def tile_moe_sup_lin_gelu_kernel(
+    tc, x_words, x_scales, w1, w2, gate, offs, pos1, pos2, out
+):
+    nc = tc.nc
+    with ExitStack() as ctx:
+        keep = ctx.enter_context(tc.tile_pool(name="keep", bufs=1))
+        psum = ctx.enter_context(tc.psum_pool(name="psum", bufs=8))
+
+        slot_list = keep.tile([P, S // 16], U16, name="slot_list")
+        pos_lists = [keep.tile([P, T // 16], U16, name="pos_list%d" % r) for r in range(2)]
+        x_codes = keep.tile([P, T], U32, name="x_codes", align_bytes=64)
+        x_plane = keep.tile([P, T], U8, name="x_plane", align_bytes=64)
+        w1_raw = keep.tile([P, 4, H], F32, name="w1_raw")
+        w1_bf = keep.tile([P, 4, P, 4], BF16, name="w1_bf", align_bytes=64)
+        w1_codes = keep.tile([P, 4, P], U32, name="w1_codes", align_bytes=64)
+        w1_plane = keep.tile([P, 4, P], U8, name="w1_plane", align_bytes=64)
+        w2_raw = [keep.tile([P, 4, N], F32, name="w2_raw%d" % e, tag="room%d" % e, align_bytes=64) for e in range(SPLIT)]
+        w2_half = {
+            (b, e): keep.tile([P, 4, P], F32, name="w2_half%d_%d" % (b, e), tag="room%d_%d" % (b, e), align_bytes=64)
+            for b in range(2)
+            for e in range(SPLIT, E)
+        }
+        w2_bf = keep.tile([P, 2, E, P, 4], BF16, name="w2_bf", align_bytes=64)
+        last_bf = keep.tile([P, 1, P, 4], BF16, name="last_bf", tag="room_last", align_bytes=64)
+        w2_codes = keep.tile([P, 2, E, P], U32, name="w2_codes", align_bytes=64)
+        w2_plane = keep.tile([P, 2, E, P], U8, name="w2_plane", align_bytes=64)
+        h_pairs = [keep.tile([P, T, 2], BF16, name="h_pairs%d" % u, align_bytes=64) for u in range(2)]
+        picked = keep.tile([P, 2, S, 2], BF16, name="picked", align_bytes=64)
+        hs_codes = keep.tile([P, S], U32, name="hs_codes", align_bytes=64)
+        hs_plane = keep.tile([P, S], U8, name="hs_plane", align_bytes=64)
+        gates = keep.tile([P, 2, T], F32, name="gates")
+        terms = [keep.tile([P, 2, T], F32, name="terms%d" % b) for b in range(2)]
+        res = keep.tile([P, 2, T], F32, name="res")
+
+        w1_rows = w1.rearrange("(p j) c -> p j c", j=4)
+        for a in range(2):
+            cols = slice(a * H // 2, (a + 1) * H // 2)
+            nc.sync.dma_start(out=w1_raw[:, :, cols], in_=w1_rows[:, :, cols])
+        nc.vector.memset(x_plane[:].bitcast(I32), 0)
+        for q in range(4):
+            nc.scalar.dma_start(
+                out=x_plane[32 * q : 32 * q + 4, :].bitcast(I32), in_=x_scales[0, 4 * q : 4 * q + 4, :].bitcast(I32)
+            )
+        x_rows = x_words[0].rearrange("p t d -> p (t d)").bitcast(I32)
+        for a in range(2):
+            toks = slice(a * T // 2, (a + 1) * T // 2)
+            nc.sync.dma_start(out=x_codes[:, toks].bitcast(I32), in_=x_rows[:, toks])
+        nc.sync.dma_start(slot_list[:], offs)
+        gate_rows = gate.rearrange("r p t -> p r t")
+        for e in range(SPLIT):
+            nc.sync.dma_start(out=w2_raw[e][:], in_=w2[e].rearrange("(p j) n -> p j n", j=4))
+            if e == 3:
+                nc.sync.dma_start(pos_lists[0][:], pos1)
+                nc.sync.dma_start(pos_lists[1][:], pos2)
+        for b in range(2):
+            for e in range(SPLIT, E):
+                nc.sync.dma_start(
+                    out=w2_half[(b, e)][:], in_=w2[e].rearrange("(p j) n -> p j n", j=4)[:, :, b * P : (b + 1) * P]
+                )
+            toks = slice(b * T // 2, (b + 1) * T // 2)
+            nc.sync.dma_start(out=gates[:, :, toks], in_=gate_rows[:, :, toks])
+
+        for a in range(2):
+            ms = slice(a * P // 2, (a + 1) * P // 2)
+            nc.vector.tensor_copy(
+                out=w1_bf[:].rearrange("p t m j -> p m t j")[:, ms],
+                in_=w1_raw[:].rearrange("p j (m t) -> p m t j", t=4)[:, ms],
+            )
+        for u in range(2):
+            ts = slice(2 * u, 2 * u + 2)
+            nc.vector.quantize_mx(
+                out=w1_codes[:, ts].rearrange("p t m -> p (t m)").bitcast(FP8X4),
+                scales=w1_plane[:, ts].rearrange("p t m -> p (t m)"),
+                in_=w1_bf[:, ts].rearrange("p t m j -> p (t m j)"),
+            )
+        for u in range(2):
+            for c in range(T // TOK):
+                toks = slice(c * TOK, (c + 1) * TOK)
+                bank = psum.tile([P, 2, TOK], F32, name="bank")
+                for d in range(2):
+                    nc.tensor.matmul_mx(
+                        out=bank[:, d, :],
+                        lhsT=w1_codes[:, 2 * u + d, :].bitcast(FP8X4),
+                        lhsT_scale=w1_plane[:, 2 * u + d, :],
+                        rhs=x_codes[:, toks].bitcast(FP8X4),
+                        rhs_scale=x_plane[:, toks],
+                        start=True,
+                        stop=True,
+                    )
+                nc.scalar.activation(out=h_pairs[u][:, toks, :], in_=bank[:].rearrange("p d t -> p t d"), func=GELU)
+
+        late = {}
+        hs_bf = {}
+        y = {}
+
+        def staged(b, lo, hi):
+            if b == 0 and lo == E - 1:
+                return last_bf[:]
+            if b == 1 and lo >= LATE:
+                if not late:
+                    late[0] = keep.tile(
+                        [P, E - LATE, P, 4], BF16, name="late_bf", tag="room0_%d" % (E - 1), align_bytes=64
+                    )
+                return late[0][:, lo - LATE : hi - LATE]
+            return w2_bf[:, b, lo:hi]
+
+        def cast_whole(e, engine):
+            if engine == "gpsimd":
+                nc.gpsimd.tensor_scalar(
+                    w2_bf[:, :, e], w2_raw[e][:].rearrange("p j (b n) -> p b n j", b=2), 1.0, 0.0, MULT, ADD
+                )
+            else:
+                copy = nc.vector.tensor_copy if engine == "vector" else nc.scalar.copy
+                copy(
+                    out=w2_bf[:, :, e].rearrange("p b (c i) j -> p b c j i", i=4),
+                    in_=w2_raw[e][:].rearrange("p j (b c i) -> p b c j i", b=2, i=4),
+                )
+
+        def cast_half(b, e):
+            src = w2_half[(b, e)][:] if e >= SPLIT else w2_raw[e][:, :, b * P : (b + 1) * P]
+            nc.scalar.copy(
+                out=staged(b, e, e + 1)[:, 0].rearrange("p (c i) j -> p c j i", i=4),
+                in_=src.rearrange("p j (c i) -> p c j i", i=4),
+            )
+
+        def quantise_w2(b, lo, hi):
+            nc.vector.quantize_mx(
+                out=w2_codes[:, b, lo:hi].rearrange("p e n -> p (e n)").bitcast(FP8X4),
+                scales=w2_plane[:, b, lo:hi].rearrange("p e n -> p (e n)"),
+                in_=staged(b, lo, hi).rearrange("p e n j -> p (e n j)"),
+            )
+
+        def gather(u, g):
+            nc.vector.tensor_copy(
+                picked[:, u, g * GS : (g + 1) * GS, :].rearrange("p s d -> p (s d)").bitcast(U32),
+                h_pairs[u][:].rearrange("p t d -> p (t d)").bitcast(U32).indirect(
+                    slot_list[:, g * GS // 16 : (g + 1) * GS // 16]
+                ),
+            )
+
+        def interleave(g, tag):
+            hs_bf[g] = keep.tile([P, GS, 4], BF16, name="hs_bf%d" % g, tag=tag, align_bytes=64)
+            nc.scalar.copy(
+                out=hs_bf[g][:].bitcast(U32),
+                in_=picked[:, :, g * GS : (g + 1) * GS, :].bitcast(U32).rearrange("p u s d -> p s (u d)"),
+            )
+
+        def quantise_h(g):
+            slots = slice(g * GS, (g + 1) * GS)
+            nc.vector.quantize_mx(
+                out=hs_codes[:, slots].bitcast(FP8X4),
+                scales=hs_plane[:, slots],
+                in_=hs_bf[g][:].rearrange("p s j -> p (s j)"),
+            )
+
+        def experts(b, lo, hi):
+            if b not in y:
+                y[b] = keep.tile([P, S], F32, name="y%d" % b, tag=("room10", "room_last")[b], align_bytes=64)
+            bank = psum.tile([P, GROUP, C], F32, name="bank")
+            for e in range(lo, hi):
+                nc.tensor.matmul_mx(
+                    out=bank[:, e - lo, :],
+                    lhsT=w2_codes[:, b, e].bitcast(FP8X4),
+                    lhsT_scale=w2_plane[:, b, e],
+                    rhs=hs_codes[:, e * C : (e + 1) * C].bitcast(FP8X4),
+                    rhs_scale=hs_plane[:, e * C : (e + 1) * C],
+                    start=True,
+                    stop=True,
+                )
+            nc.scalar.copy(
+                out=y[b][:, lo * C : hi * C], in_=bank[:, 0 : hi - lo, :].rearrange("p e c -> p (e c)")
+            )
+
+        for g0 in (0, 2):
+            if g0 == 0:
+                for u, g in ((0, 0), (0, 1), (1, 0), (1, 1)):
+                    gather(u, g)
+            else:
+                for u, g in ((0, 2), (1, 2), (0, 3), (1, 3)):
+                    gather(u, g)
+
+        cast_whole(0, "vector")
+        quantise_w2(0, 0, 1)
+        quantise_w2(1, 0, 1)
+        for e in (1, 2, 4, 5, 6, 8):
+            cast_whole(e, "gpsimd")
+        cast_whole(3, "scalar")
+        interleave(0, "hs0")
+        interleave(1, "hs1")
+        cast_whole(7, "scalar")
+        interleave(2, "room7")
+        cast_whole(9, "scalar")
+        interleave(3, "room9")
+        cast_whole(10, "scalar")
+
+        quantise_h(0)
+        quantise_w2(0, 1, 2)
+        quantise_w2(0, 2, 4)
+        experts(0, 0, 4)
+        quantise_h(1)
+        quantise_w2(0, 4, 8)
+        experts(0, 4, 8)
+        quantise_h(2)
+        quantise_w2(0, 8, 10)
+        quantise_h(3)
+        cast_half(0, 11)
+        quantise_w2(0, 10, 12)
+        cast_half(0, 12)
+        cast_half(0, 13)
+        quantise_w2(0, 12, 14)
+        experts(0, 8, 12)
+        cast_half(0, 14)
+        quantise_w2(0, 14, 15)
+        cast_half(0, 15)
+        quantise_w2(0, 15, 16)
+        experts(0, 12, 16)
+
+        quantise_w2(1, 1, 2)
+        quantise_w2(1, 2, 4)
+        quantise_w2(1, 4, 8)
+        quantise_w2(1, 8, 10)
+        quantise_w2(1, 10, 11)
+        cast_half(1, 11)
+        cast_half(1, 12)
+        quantise_w2(1, 11, 13)
+        cast_half(1, 13)
+        cast_half(1, 14)
+        quantise_w2(1, 13, 15)
+        cast_half(1, 15)
+        quantise_w2(1, 15, 16)
+        for g in range(4):
+            experts(1, 4 * g, 4 * g + 4)
+
+        pieces = []
+        for b in range(2):
+            lo = 0
+            for width in PIECES[b]:
+                pieces.append((b, lo, lo + width))
+                lo += width
+
+        def product(piece, r):
+            b, lo, hi = piece
+            nc.vector.tensor_tensor(
+                terms[r][:, b, lo:hi], y[b][:].indirect(pos_lists[r][:, lo // 16 : hi // 16]), gates[:, r, lo:hi], MULT
+            )
+
+        def finish(piece):
+            b, lo, hi = piece
+            nc.vector.tensor_tensor(res[:, b, lo:hi], terms[0][:, b, lo:hi], terms[1][:, b, lo:hi], ADD)
+            nc.sync.dma_start(out=out[b * P : (b + 1) * P, lo:hi], in_=res[:, b, lo:hi])
+
+        for i, piece in enumerate(pieces):
+            product(piece, 0)
+            if i > 0:
+                finish(pieces[i - 1])
+            product(piece, 1)
+        finish(pieces[-1])

@@ -23,6 +23,8 @@ GROUP = 4
 GS = GROUP * C
 SPLIT = 14
 LATE = 11
+EARLY = 2
+WHOLE = ((0, 2), (2, 9), (9, 11))
 PIECES = ((512, 512), (512, 256, 256))
 
 
@@ -38,7 +40,7 @@ def tile_moe_sup_lin_gelu_kernel(
         pos_lists = [keep.tile([P, T // 16], U16, name="pos_list%d" % r) for r in range(2)]
         x_codes = keep.tile([P, T], U32, name="x_codes", align_bytes=64)
         x_plane = keep.tile([P, T], U8, name="x_plane", align_bytes=64)
-        w1_raw = keep.tile([P, 4, H], F32, name="w1_raw")
+        w1_raw = [keep.tile([P, 4, H // 2], F32, name="w1_raw%d" % a) for a in range(2)]
         w1_bf = keep.tile([P, 4, P, 4], BF16, name="w1_bf", align_bytes=64)
         w1_codes = keep.tile([P, 4, P], U32, name="w1_codes", align_bytes=64)
         w1_plane = keep.tile([P, 4, P], U8, name="w1_plane", align_bytes=64)
@@ -48,35 +50,35 @@ def tile_moe_sup_lin_gelu_kernel(
             for b in range(2)
             for e in range(SPLIT, E)
         }
-        w2_bf = keep.tile([P, 2, E, P, 4], BF16, name="w2_bf", align_bytes=64)
+        whole_bf = {
+            lo: keep.tile([P, 2, hi - lo, P, 4], BF16, name="whole_bf%d" % lo, align_bytes=64) for lo, hi in WHOLE
+        }
+        first_bf = keep.tile([P, E - 1 - LATE, P, 4], BF16, name="first_bf", align_bytes=64)
         last_bf = keep.tile([P, 1, P, 4], BF16, name="last_bf", tag="room_last", align_bytes=64)
-        w2_codes = keep.tile([P, 2, E, P], U32, name="w2_codes", align_bytes=64)
+        w2_codes = keep.tile([P, E + EARLY, P], U32, name="w2_codes", align_bytes=64)
         w2_plane = keep.tile([P, 2, E, P], U8, name="w2_plane", align_bytes=64)
         h_pairs = [keep.tile([P, T, 2], BF16, name="h_pairs%d" % u, align_bytes=64) for u in range(2)]
-        picked = keep.tile([P, 2, S, 2], BF16, name="picked", align_bytes=64)
+        picked = [keep.tile([P, 2, GS, 2], BF16, name="picked%d" % g, align_bytes=64) for g in range(E // GROUP)]
         hs_codes = keep.tile([P, S], U32, name="hs_codes", align_bytes=64)
         hs_plane = keep.tile([P, S], U8, name="hs_plane", align_bytes=64)
-        gates = keep.tile([P, 2, T], F32, name="gates")
-        terms = [keep.tile([P, 2, T], F32, name="terms%d" % b) for b in range(2)]
+        gates = [keep.tile([P, 2, T // 2], F32, name="gates%d" % a) for a in range(2)]
         res = keep.tile([P, 2, T], F32, name="res")
 
         w1_rows = w1.rearrange("(p j) c -> p j c", j=4)
         for a in range(2):
             cols = slice(a * H // 2, (a + 1) * H // 2)
-            nc.sync.dma_start(out=w1_raw[:, :, cols], in_=w1_rows[:, :, cols])
+            nc.sync.dma_start(out=w1_raw[a][:], in_=w1_rows[:, :, cols])
         nc.vector.memset(x_plane[:].bitcast(I32), 0)
         for q in range(4):
-            nc.scalar.dma_start(
+            nc.sync.dma_start(
                 out=x_plane[32 * q : 32 * q + 4, :].bitcast(I32), in_=x_scales[0, 4 * q : 4 * q + 4, :].bitcast(I32)
             )
-        x_rows = x_words[0].rearrange("p t d -> p (t d)").bitcast(I32)
-        for a in range(2):
-            toks = slice(a * T // 2, (a + 1) * T // 2)
-            nc.sync.dma_start(out=x_codes[:, toks].bitcast(I32), in_=x_rows[:, toks])
-        nc.sync.dma_start(slot_list[:], offs)
+        nc.sync.dma_start(out=x_codes[:].bitcast(I32), in_=x_words[0].rearrange("p t d -> p (t d)").bitcast(I32))
         gate_rows = gate.rearrange("r p t -> p r t")
-        for e in range(SPLIT):
+        for e in (0, 1, 2, 3, 9, 4, 5, 6, 7, 8, 10, 11, 12, 13):
             nc.sync.dma_start(out=w2_raw[e][:], in_=w2[e].rearrange("(p j) n -> p j n", j=4))
+            if e == 0:
+                nc.sync.dma_start(slot_list[:], offs)
             if e == 3:
                 nc.sync.dma_start(pos_lists[0][:], pos1)
                 nc.sync.dma_start(pos_lists[1][:], pos2)
@@ -86,13 +88,13 @@ def tile_moe_sup_lin_gelu_kernel(
                     out=w2_half[(b, e)][:], in_=w2[e].rearrange("(p j) n -> p j n", j=4)[:, :, b * P : (b + 1) * P]
                 )
             toks = slice(b * T // 2, (b + 1) * T // 2)
-            nc.sync.dma_start(out=gates[:, :, toks], in_=gate_rows[:, :, toks])
+            nc.sync.dma_start(out=gates[b][:], in_=gate_rows[:, :, toks])
 
         for a in range(2):
             ms = slice(a * P // 2, (a + 1) * P // 2)
             nc.vector.tensor_copy(
                 out=w1_bf[:].rearrange("p t m j -> p m t j")[:, ms],
-                in_=w1_raw[:].rearrange("p j (m t) -> p m t j", t=4)[:, ms],
+                in_=w1_raw[a][:].rearrange("p j (m t) -> p m t j", t=4),
             )
         for u in range(2):
             ts = slice(2 * u, 2 * u + 2)
@@ -121,57 +123,81 @@ def tile_moe_sup_lin_gelu_kernel(
         hs_bf = {}
         y = {}
 
+        late_codes = {}
+
+        def codes(b, lo, hi):
+            if b == 0:
+                return w2_codes[:, lo:hi]
+            if hi <= EARLY:
+                return w2_codes[:, E + lo : E + hi]
+            if not late_codes:
+                late_codes[0] = keep.tile([P, E - EARLY, P], U32, name="late_codes", tag="room_last", align_bytes=64)
+            return late_codes[0][:, lo - EARLY : hi - EARLY]
+
         def staged(b, lo, hi):
             if b == 0 and lo == E - 1:
                 return last_bf[:]
             if b == 1 and lo >= LATE:
                 if not late:
                     late[0] = keep.tile(
-                        [P, E - LATE, P, 4], BF16, name="late_bf", tag="room0_%d" % (E - 1), align_bytes=64
+                        [P, E - LATE, P, 4], BF16, name="late_bf", tag="room0_%d" % (E - 2), align_bytes=64
                     )
                 return late[0][:, lo - LATE : hi - LATE]
-            return w2_bf[:, b, lo:hi]
+            if lo >= LATE:
+                return first_bf[:, lo - LATE : hi - LATE]
+            start = max(s for s, end in WHOLE if s <= lo)
+            return whole_bf[start][:, b, lo - start : hi - start]
+
+        def cast_half(b, e, engine="scalar"):
+            src = w2_half[(b, e)][:] if e >= SPLIT else w2_raw[e][:, :, b * P : (b + 1) * P]
+            dst = staged(b, e, e + 1)[:, 0]
+            if engine == "gpsimd":
+                nc.gpsimd.tensor_scalar(dst, src.rearrange("p j n -> p n j"), 1.0, 0.0, MULT, ADD)
+            else:
+                copy = nc.vector.tensor_copy if engine == "vector" else nc.scalar.copy
+                copy(out=dst.rearrange("p (c i) j -> p c j i", i=4), in_=src.rearrange("p j (c i) -> p c j i", i=4))
 
         def cast_whole(e, engine):
+            start = max(s for s, end in WHOLE if s <= e)
+            dst = whole_bf[start][:, :, e - start]
             if engine == "gpsimd":
                 nc.gpsimd.tensor_scalar(
-                    w2_bf[:, :, e], w2_raw[e][:].rearrange("p j (b n) -> p b n j", b=2), 1.0, 0.0, MULT, ADD
+                    dst, w2_raw[e][:].rearrange("p j (b n) -> p b n j", b=2), 1.0, 0.0, MULT, ADD
                 )
             else:
                 copy = nc.vector.tensor_copy if engine == "vector" else nc.scalar.copy
                 copy(
-                    out=w2_bf[:, :, e].rearrange("p b (c i) j -> p b c j i", i=4),
+                    out=dst.rearrange("p b (c i) j -> p b c j i", i=4),
                     in_=w2_raw[e][:].rearrange("p j (b c i) -> p b c j i", b=2, i=4),
                 )
 
-        def cast_half(b, e):
-            src = w2_half[(b, e)][:] if e >= SPLIT else w2_raw[e][:, :, b * P : (b + 1) * P]
-            nc.scalar.copy(
-                out=staged(b, e, e + 1)[:, 0].rearrange("p (c i) j -> p c j i", i=4),
-                in_=src.rearrange("p j (c i) -> p c j i", i=4),
-            )
-
         def quantise_w2(b, lo, hi):
             nc.vector.quantize_mx(
-                out=w2_codes[:, b, lo:hi].rearrange("p e n -> p (e n)").bitcast(FP8X4),
+                out=codes(b, lo, hi).rearrange("p e n -> p (e n)").bitcast(FP8X4),
                 scales=w2_plane[:, b, lo:hi].rearrange("p e n -> p (e n)"),
                 in_=staged(b, lo, hi).rearrange("p e n j -> p (e n j)"),
             )
 
         def gather(u, g):
             nc.vector.tensor_copy(
-                picked[:, u, g * GS : (g + 1) * GS, :].rearrange("p s d -> p (s d)").bitcast(U32),
+                picked[g][:, u].rearrange("p s d -> p (s d)").bitcast(U32),
                 h_pairs[u][:].rearrange("p t d -> p (t d)").bitcast(U32).indirect(
                     slot_list[:, g * GS // 16 : (g + 1) * GS // 16]
                 ),
             )
 
-        def interleave(g, tag):
+        def interleave(g, tag, engine="scalar"):
             hs_bf[g] = keep.tile([P, GS, 4], BF16, name="hs_bf%d" % g, tag=tag, align_bytes=64)
-            nc.scalar.copy(
-                out=hs_bf[g][:].bitcast(U32),
-                in_=picked[:, :, g * GS : (g + 1) * GS, :].bitcast(U32).rearrange("p u s d -> p s (u d)"),
-            )
+            if engine == "scalar":
+                nc.scalar.copy(
+                    out=hs_bf[g][:].bitcast(U32),
+                    in_=picked[g][:].bitcast(U32).rearrange("p u s d -> p s (u d)"),
+                )
+            else:
+                nc.vector.tensor_copy(
+                    out=hs_bf[g][:].rearrange("p s (u d) -> p s u d", u=2),
+                    in_=picked[g][:].rearrange("p u s d -> p s u d"),
+                )
 
         def quantise_h(g):
             slots = slice(g * GS, (g + 1) * GS)
@@ -183,12 +209,12 @@ def tile_moe_sup_lin_gelu_kernel(
 
         def experts(b, lo, hi):
             if b not in y:
-                y[b] = keep.tile([P, S], F32, name="y%d" % b, tag=("room10", "room_last")[b], align_bytes=64)
+                y[b] = keep.tile([P, S], F32, name="y%d" % b, tag=("room0_%d" % (E - 1), "y1")[b], align_bytes=64)
             bank = psum.tile([P, GROUP, C], F32, name="bank")
             for e in range(lo, hi):
                 nc.tensor.matmul_mx(
                     out=bank[:, e - lo, :],
-                    lhsT=w2_codes[:, b, e].bitcast(FP8X4),
+                    lhsT=codes(b, e, e + 1)[:, 0].bitcast(FP8X4),
                     lhsT_scale=w2_plane[:, b, e],
                     rhs=hs_codes[:, e * C : (e + 1) * C].bitcast(FP8X4),
                     rhs_scale=hs_plane[:, e * C : (e + 1) * C],
@@ -208,46 +234,40 @@ def tile_moe_sup_lin_gelu_kernel(
                     gather(u, g)
 
         cast_whole(0, "vector")
-        quantise_w2(0, 0, 1)
-        quantise_w2(1, 0, 1)
-        for e in (1, 2, 4, 5, 6, 8):
+        cast_whole(1, "vector")
+        quantise_w2(0, 0, 2)
+        quantise_w2(1, 0, 2)
+        for e in range(2, 9):
             cast_whole(e, "gpsimd")
-        cast_whole(3, "scalar")
+        cast_whole(9, "scalar")
         interleave(0, "hs0")
         interleave(1, "hs1")
-        cast_whole(7, "scalar")
-        interleave(2, "room7")
-        cast_whole(9, "scalar")
-        interleave(3, "room9")
+        interleave(2, "room9")
         cast_whole(10, "scalar")
+        interleave(3, "room10")
 
+        for e in range(11, E):
+            cast_half(0, e)
         quantise_h(0)
-        quantise_w2(0, 1, 2)
         quantise_w2(0, 2, 4)
         experts(0, 0, 4)
         quantise_h(1)
         quantise_w2(0, 4, 8)
         experts(0, 4, 8)
         quantise_h(2)
-        quantise_w2(0, 8, 10)
-        quantise_h(3)
-        cast_half(0, 11)
-        quantise_w2(0, 10, 12)
-        cast_half(0, 12)
-        cast_half(0, 13)
-        quantise_w2(0, 12, 14)
+        quantise_w2(0, 8, 9)
+        quantise_w2(0, 9, 11)
+        quantise_w2(0, 11, 13)
         experts(0, 8, 12)
-        cast_half(0, 14)
-        quantise_w2(0, 14, 15)
-        cast_half(0, 15)
+        quantise_h(3)
+        quantise_w2(0, 13, 15)
         quantise_w2(0, 15, 16)
         experts(0, 12, 16)
 
-        quantise_w2(1, 1, 2)
         quantise_w2(1, 2, 4)
         quantise_w2(1, 4, 8)
-        quantise_w2(1, 8, 10)
-        quantise_w2(1, 10, 11)
+        quantise_w2(1, 8, 9)
+        quantise_w2(1, 9, 11)
         cast_half(1, 11)
         cast_half(1, 12)
         quantise_w2(1, 11, 13)
@@ -266,15 +286,19 @@ def tile_moe_sup_lin_gelu_kernel(
                 pieces.append((b, lo, lo + width))
                 lo += width
 
+        terms = {}
+
         def product(piece, r):
             b, lo, hi = piece
+            tag = "room0_%d" % (E - 2) if (b, hi, r) == (0, T, 1) else "term%d_%d_%d" % (b, lo, r)
+            terms[(piece, r)] = keep.tile([P, hi - lo], F32, name="term%d_%d_%d" % (b, lo, r), tag=tag, align_bytes=64)
             nc.vector.tensor_tensor(
-                terms[r][:, b, lo:hi], y[b][:].indirect(pos_lists[r][:, lo // 16 : hi // 16]), gates[:, r, lo:hi], MULT
+                terms[(piece, r)][:], y[b][:].indirect(pos_lists[r][:, lo // 16 : hi // 16]), gates[lo // (T // 2)][:, r, lo % (T // 2) : lo % (T // 2) + hi - lo], MULT
             )
 
         def finish(piece):
             b, lo, hi = piece
-            nc.vector.tensor_tensor(res[:, b, lo:hi], terms[0][:, b, lo:hi], terms[1][:, b, lo:hi], ADD)
+            nc.vector.tensor_tensor(res[:, b, lo:hi], terms[(piece, 0)][:], terms[(piece, 1)][:], ADD)
             nc.sync.dma_start(out=out[b * P : (b + 1) * P, lo:hi], in_=res[:, b, lo:hi])
 
         for i, piece in enumerate(pieces):

@@ -1,6 +1,7 @@
 from contextlib import ExitStack
 
 import concourse.mybir as mybir
+from concourse.masks import make_identity
 
 K, T, E, C, H, N = 512, 1024, 16, 128, 512, 256
 S = E * C
@@ -18,14 +19,22 @@ ADD = mybir.AluOpType.add
 GELU = mybir.ActivationFunctionType.Gelu_apprx_tanh
 
 P = 128
-TOK = 256
+BANKS = 8
+BANK_TOKENS = 256
 GROUP = 4
-GS = GROUP * C
-SPLIT = 14
-LATE = 11
-EARLY = 2
-WHOLE = ((0, 2), (2, 9), (9, 11))
-PIECES = ((512, 512), (512, 256, 256))
+GROUP_SLOTS = GROUP * C
+GROUPS = E // GROUP
+
+ON_VECTOR = 2
+HALVED = 9
+DEFERRED = HALVED + 1
+SPLIT_LOAD = 14
+LAST = E - 1
+CODES_CUT = 13
+DEFERRED_CUT = 14
+
+PIECE_WIDTHS = ((512, 512), (512, 256, 256))
+TURNED = 2
 
 
 def tile_moe_sup_lin_gelu_kernel(
@@ -34,187 +43,152 @@ def tile_moe_sup_lin_gelu_kernel(
     nc = tc.nc
     with ExitStack() as ctx:
         keep = ctx.enter_context(tc.tile_pool(name="keep", bufs=1))
-        psum = ctx.enter_context(tc.psum_pool(name="psum", bufs=8))
+        psum = ctx.enter_context(tc.psum_pool(name="psum", bufs=BANKS))
+
+        def sbuf(shape, dtype, name, tag=None):
+            return keep.tile(shape, dtype, name=name, tag=tag or name, align_bytes=64)
 
         slot_list = keep.tile([P, S // 16], U16, name="slot_list")
         pos_lists = [keep.tile([P, T // 16], U16, name="pos_list%d" % r) for r in range(2)]
-        x_codes = keep.tile([P, T], U32, name="x_codes", align_bytes=64)
-        x_plane = keep.tile([P, T], U8, name="x_plane", align_bytes=64)
-        w1_raw = [keep.tile([P, 4, H // 2], F32, name="w1_raw%d" % a) for a in range(2)]
-        w1_bf = keep.tile([P, 4, P, 4], BF16, name="w1_bf", align_bytes=64)
-        w1_codes = keep.tile([P, 4, P], U32, name="w1_codes", align_bytes=64)
-        w1_plane = keep.tile([P, 4, P], U8, name="w1_plane", align_bytes=64)
-        w2_raw = [keep.tile([P, 4, N], F32, name="w2_raw%d" % e, tag="room%d" % e, align_bytes=64) for e in range(SPLIT)]
-        w2_half = {
-            (b, e): keep.tile([P, 4, P], F32, name="w2_half%d_%d" % (b, e), tag="room%d_%d" % (b, e), align_bytes=64)
-            for b in range(2)
-            for e in range(SPLIT, E)
+        ident = sbuf([P, P], F32, "ident")
+        x_codes = sbuf([P, T], U32, "x_codes")
+        x_plane = sbuf([P, T], U8, "x_plane")
+        w1_raw = [sbuf([P, 4, H // 2], F32, "w1_raw%d" % a) for a in range(2)]
+        w1_bf = sbuf([P, 4, P, 4], BF16, "w1_bf")
+        w1_codes = sbuf([P, 4, P], U32, "w1_codes")
+        w1_plane = sbuf([P, 4, P], U8, "w1_plane")
+        h_pairs = [sbuf([P, T, 2], BF16, "h_pairs%d" % u) for u in range(2)]
+        picked = [sbuf([P, 2, GROUP_SLOTS, 2], BF16, "picked%d" % g) for g in range(GROUPS)]
+        hs_bf = [sbuf([P, GROUP_SLOTS, 4], BF16, "hs_bf%d" % g) for g in range(GROUPS)]
+        hs_codes = sbuf([P, S], U32, "hs_codes")
+        hs_plane = sbuf([P, S], U8, "hs_plane")
+        w2_plane = sbuf([P, 2, E, P], U8, "w2_plane")
+        gates = [sbuf([P, 2, T // 2], F32, "gates%d" % a) for a in range(2)]
+        res = sbuf([P, 2, T], F32, "res")
+
+        w2_whole = [sbuf([P, 4, N], F32, "w2_whole%d" % e) for e in range(SPLIT_LOAD)]
+        w2_raw = {(b, e): w2_whole[e][:, :, b * P : (b + 1) * P] for b in range(2) for e in range(SPLIT_LOAD)}
+        for b in range(2):
+            for e in range(SPLIT_LOAD, E):
+                w2_raw[(b, e)] = sbuf([P, 4, P], F32, "w2_half%d_%d" % (b, e))[:]
+
+        both_bf = {
+            lo: sbuf([P, 2, hi - lo, P, 4], BF16, "both_bf%d" % lo) for lo, hi in ((0, ON_VECTOR), (ON_VECTOR, HALVED))
         }
-        whole_bf = {
-            lo: keep.tile([P, 2, hi - lo, P, 4], BF16, name="whole_bf%d" % lo, align_bytes=64) for lo, hi in WHOLE
-        }
-        first_bf = keep.tile([P, E - 1 - LATE, P, 4], BF16, name="first_bf", align_bytes=64)
-        last_bf = keep.tile([P, 1, P, 4], BF16, name="last_bf", tag="room_last", align_bytes=64)
-        w2_codes = keep.tile([P, E + EARLY, P], U32, name="w2_codes", align_bytes=64)
-        w2_plane = keep.tile([P, 2, E, P], U8, name="w2_plane", align_bytes=64)
-        h_pairs = [keep.tile([P, T, 2], BF16, name="h_pairs%d" % u, align_bytes=64) for u in range(2)]
-        picked = [keep.tile([P, 2, GS, 2], BF16, name="picked%d" % g, align_bytes=64) for g in range(E // GROUP)]
-        hs_codes = keep.tile([P, S], U32, name="hs_codes", align_bytes=64)
-        hs_plane = keep.tile([P, S], U8, name="hs_plane", align_bytes=64)
-        gates = [keep.tile([P, 2, T // 2], F32, name="gates%d" % a) for a in range(2)]
-        res = keep.tile([P, 2, T], F32, name="res")
+        bf_runs = [(b, lo, lo + tile.shape[2], tile[:, b]) for lo, tile in both_bf.items() for b in range(2)]
+        bf_runs.append((0, HALVED, LAST, sbuf([P, LAST - HALVED, P, 4], BF16, "half0_bf")[:]))
+        bf_runs.append((0, LAST, E, sbuf([P, 1, P, 4], BF16, "last_bf", "after_half0_codes")[:]))
+        bf_runs.append((1, HALVED, DEFERRED, sbuf([P, 1, P, 4], BF16, "vector_half1_bf")[:]))
+        code_runs = [
+            (0, 0, HALVED, sbuf([P, HALVED, P], U32, "early_codes0")[:]),
+            (0, HALVED, CODES_CUT, sbuf([P, CODES_CUT - HALVED, P], U32, "late_codes0", "second_deferred")[:]),
+            (0, CODES_CUT, E, sbuf([P, E - CODES_CUT, P], U32, "last_codes0", "first_deferred")[:]),
+            (1, 0, ON_VECTOR, sbuf([P, ON_VECTOR, P], U32, "early_codes1")[:]),
+        ]
+
+        def experts_of(runs, b, lo, hi):
+            first, view = [(first, view) for half, first, end, view in runs if half == b and first <= lo < end][0]
+            return view[:, lo - first : hi - first]
+
+        make_identity(nc, ident[:])
 
         w1_rows = w1.rearrange("(p j) c -> p j c", j=4)
         for a in range(2):
-            cols = slice(a * H // 2, (a + 1) * H // 2)
-            nc.sync.dma_start(out=w1_raw[a][:], in_=w1_rows[:, :, cols])
+            nc.sync.dma_start(out=w1_raw[a][:], in_=w1_rows[:, :, a * H // 2 : (a + 1) * H // 2])
         nc.vector.memset(x_plane[:].bitcast(I32), 0)
         for q in range(4):
             nc.sync.dma_start(
                 out=x_plane[32 * q : 32 * q + 4, :].bitcast(I32), in_=x_scales[0, 4 * q : 4 * q + 4, :].bitcast(I32)
             )
         nc.sync.dma_start(out=x_codes[:].bitcast(I32), in_=x_words[0].rearrange("p t d -> p (t d)").bitcast(I32))
-        gate_rows = gate.rearrange("r p t -> p r t")
-        for e in (0, 1, 2, 3, 9, 4, 5, 6, 7, 8, 10, 11, 12, 13):
-            nc.sync.dma_start(out=w2_raw[e][:], in_=w2[e].rearrange("(p j) n -> p j n", j=4))
+        w2_rows = [w2[e].rearrange("(p j) n -> p j n", j=4) for e in range(E)]
+        for e in range(SPLIT_LOAD):
+            nc.sync.dma_start(out=w2_whole[e][:], in_=w2_rows[e])
             if e == 0:
                 nc.sync.dma_start(slot_list[:], offs)
-            if e == 3:
+            if e == GROUP - 1:
                 nc.sync.dma_start(pos_lists[0][:], pos1)
                 nc.sync.dma_start(pos_lists[1][:], pos2)
+        gate_rows = gate.rearrange("r p t -> p r t")
         for b in range(2):
-            for e in range(SPLIT, E):
-                nc.sync.dma_start(
-                    out=w2_half[(b, e)][:], in_=w2[e].rearrange("(p j) n -> p j n", j=4)[:, :, b * P : (b + 1) * P]
-                )
-            toks = slice(b * T // 2, (b + 1) * T // 2)
-            nc.sync.dma_start(out=gates[b][:], in_=gate_rows[:, :, toks])
+            for e in range(SPLIT_LOAD, E):
+                nc.sync.dma_start(out=w2_raw[(b, e)], in_=w2_rows[e][:, :, b * P : (b + 1) * P])
+            nc.sync.dma_start(out=gates[b][:], in_=gate_rows[:, :, b * T // 2 : (b + 1) * T // 2])
 
         for a in range(2):
-            ms = slice(a * P // 2, (a + 1) * P // 2)
             nc.vector.tensor_copy(
-                out=w1_bf[:].rearrange("p t m j -> p m t j")[:, ms],
+                out=w1_bf[:].rearrange("p t m j -> p m t j")[:, a * P // 2 : (a + 1) * P // 2],
                 in_=w1_raw[a][:].rearrange("p j (m t) -> p m t j", t=4),
             )
         for u in range(2):
-            ts = slice(2 * u, 2 * u + 2)
             nc.vector.quantize_mx(
-                out=w1_codes[:, ts].rearrange("p t m -> p (t m)").bitcast(FP8X4),
-                scales=w1_plane[:, ts].rearrange("p t m -> p (t m)"),
-                in_=w1_bf[:, ts].rearrange("p t m j -> p (t m j)"),
+                out=w1_codes[:, 2 * u : 2 * u + 2].rearrange("p t m -> p (t m)").bitcast(FP8X4),
+                scales=w1_plane[:, 2 * u : 2 * u + 2].rearrange("p t m -> p (t m)"),
+                in_=w1_bf[:, 2 * u : 2 * u + 2].rearrange("p t m j -> p (t m j)"),
             )
         for u in range(2):
-            for c in range(T // TOK):
-                toks = slice(c * TOK, (c + 1) * TOK)
-                bank = psum.tile([P, 2, TOK], F32, name="bank")
+            for lo in range(0, T, BANK_TOKENS):
+                tokens = slice(lo, lo + BANK_TOKENS)
+                bank = psum.tile([P, 2, BANK_TOKENS], F32, name="bank")
                 for d in range(2):
                     nc.tensor.matmul_mx(
                         out=bank[:, d, :],
                         lhsT=w1_codes[:, 2 * u + d, :].bitcast(FP8X4),
                         lhsT_scale=w1_plane[:, 2 * u + d, :],
-                        rhs=x_codes[:, toks].bitcast(FP8X4),
-                        rhs_scale=x_plane[:, toks],
+                        rhs=x_codes[:, tokens].bitcast(FP8X4),
+                        rhs_scale=x_plane[:, tokens],
                         start=True,
                         stop=True,
                     )
-                nc.scalar.activation(out=h_pairs[u][:, toks, :], in_=bank[:].rearrange("p d t -> p t d"), func=GELU)
+                nc.scalar.activation(out=h_pairs[u][:, tokens, :], in_=bank[:].rearrange("p d t -> p t d"), func=GELU)
 
-        late = {}
-        hs_bf = {}
-        y = {}
+        def round_both(e, first, copy):
+            copy(
+                out=both_bf[first][:, :, e - first].rearrange("p b (c i) j -> p b c j i", i=4),
+                in_=w2_whole[e][:].rearrange("p j (b c i) -> p b c j i", b=2, i=4),
+            )
 
-        late_codes = {}
-
-        def codes(b, lo, hi):
-            if b == 0:
-                return w2_codes[:, lo:hi]
-            if hi <= EARLY:
-                return w2_codes[:, E + lo : E + hi]
-            if not late_codes:
-                late_codes[0] = keep.tile([P, E - EARLY, P], U32, name="late_codes", tag="room_last", align_bytes=64)
-            return late_codes[0][:, lo - EARLY : hi - EARLY]
-
-        def staged(b, lo, hi):
-            if b == 0 and lo == E - 1:
-                return last_bf[:]
-            if b == 1 and lo >= LATE:
-                if not late:
-                    late[0] = keep.tile(
-                        [P, E - LATE, P, 4], BF16, name="late_bf", tag="room0_%d" % (E - 2), align_bytes=64
-                    )
-                return late[0][:, lo - LATE : hi - LATE]
-            if lo >= LATE:
-                return first_bf[:, lo - LATE : hi - LATE]
-            start = max(s for s, end in WHOLE if s <= lo)
-            return whole_bf[start][:, b, lo - start : hi - start]
-
-        def cast_half(b, e, engine="scalar"):
-            src = w2_half[(b, e)][:] if e >= SPLIT else w2_raw[e][:, :, b * P : (b + 1) * P]
-            dst = staged(b, e, e + 1)[:, 0]
-            if engine == "gpsimd":
-                nc.gpsimd.tensor_scalar(dst, src.rearrange("p j n -> p n j"), 1.0, 0.0, MULT, ADD)
-            else:
-                copy = nc.vector.tensor_copy if engine == "vector" else nc.scalar.copy
-                copy(out=dst.rearrange("p (c i) j -> p c j i", i=4), in_=src.rearrange("p j (c i) -> p c j i", i=4))
-
-        def cast_whole(e, engine):
-            start = max(s for s, end in WHOLE if s <= e)
-            dst = whole_bf[start][:, :, e - start]
-            if engine == "gpsimd":
-                nc.gpsimd.tensor_scalar(
-                    dst, w2_raw[e][:].rearrange("p j (b n) -> p b n j", b=2), 1.0, 0.0, MULT, ADD
-                )
-            else:
-                copy = nc.vector.tensor_copy if engine == "vector" else nc.scalar.copy
-                copy(
-                    out=dst.rearrange("p b (c i) j -> p b c j i", i=4),
-                    in_=w2_raw[e][:].rearrange("p j (b c i) -> p b c j i", b=2, i=4),
-                )
+        def round_half(b, e, copy):
+            copy(
+                out=experts_of(bf_runs, b, e, e + 1)[:, 0].rearrange("p (c i) j -> p c j i", i=4),
+                in_=w2_raw[(b, e)].rearrange("p j (c i) -> p c j i", i=4),
+            )
 
         def quantise_w2(b, lo, hi):
             nc.vector.quantize_mx(
-                out=codes(b, lo, hi).rearrange("p e n -> p (e n)").bitcast(FP8X4),
+                out=experts_of(code_runs, b, lo, hi).rearrange("p e n -> p (e n)").bitcast(FP8X4),
                 scales=w2_plane[:, b, lo:hi].rearrange("p e n -> p (e n)"),
-                in_=staged(b, lo, hi).rearrange("p e n j -> p (e n j)"),
+                in_=experts_of(bf_runs, b, lo, hi).rearrange("p e n j -> p (e n j)"),
             )
 
         def gather(u, g):
             nc.vector.tensor_copy(
                 picked[g][:, u].rearrange("p s d -> p (s d)").bitcast(U32),
-                h_pairs[u][:].rearrange("p t d -> p (t d)").bitcast(U32).indirect(
-                    slot_list[:, g * GS // 16 : (g + 1) * GS // 16]
-                ),
+                h_pairs[u][:]
+                .rearrange("p t d -> p (t d)")
+                .bitcast(U32)
+                .indirect(slot_list[:, g * GROUP_SLOTS // 16 : (g + 1) * GROUP_SLOTS // 16]),
             )
 
-        def interleave(g, tag, engine="scalar"):
-            hs_bf[g] = keep.tile([P, GS, 4], BF16, name="hs_bf%d" % g, tag=tag, align_bytes=64)
-            if engine == "scalar":
-                nc.scalar.copy(
-                    out=hs_bf[g][:].bitcast(U32),
-                    in_=picked[g][:].bitcast(U32).rearrange("p u s d -> p s (u d)"),
-                )
-            else:
-                nc.vector.tensor_copy(
-                    out=hs_bf[g][:].rearrange("p s (u d) -> p s u d", u=2),
-                    in_=picked[g][:].rearrange("p u s d -> p s u d"),
-                )
+        def interleave(g):
+            nc.vector.tensor_copy(
+                out=hs_bf[g][:].rearrange("p s (u d) -> p s u d", u=2), in_=picked[g][:].rearrange("p u s d -> p s u d")
+            )
 
         def quantise_h(g):
-            slots = slice(g * GS, (g + 1) * GS)
+            slots = slice(g * GROUP_SLOTS, (g + 1) * GROUP_SLOTS)
             nc.vector.quantize_mx(
                 out=hs_codes[:, slots].bitcast(FP8X4),
                 scales=hs_plane[:, slots],
                 in_=hs_bf[g][:].rearrange("p s j -> p (s j)"),
             )
 
-        def experts(b, lo, hi):
-            if b not in y:
-                y[b] = keep.tile([P, S], F32, name="y%d" % b, tag=("room0_%d" % (E - 1), "y1")[b], align_bytes=64)
+        def multiply(b, g, y_half):
             bank = psum.tile([P, GROUP, C], F32, name="bank")
-            for e in range(lo, hi):
+            for e in range(g * GROUP, (g + 1) * GROUP):
                 nc.tensor.matmul_mx(
-                    out=bank[:, e - lo, :],
-                    lhsT=codes(b, e, e + 1)[:, 0].bitcast(FP8X4),
+                    out=bank[:, e % GROUP, :],
+                    lhsT=experts_of(code_runs, b, e, e + 1)[:, 0].bitcast(FP8X4),
                     lhsT_scale=w2_plane[:, b, e],
                     rhs=hs_codes[:, e * C : (e + 1) * C].bitcast(FP8X4),
                     rhs_scale=hs_plane[:, e * C : (e + 1) * C],
@@ -222,88 +196,116 @@ def tile_moe_sup_lin_gelu_kernel(
                     stop=True,
                 )
             nc.scalar.copy(
-                out=y[b][:, lo * C : hi * C], in_=bank[:, 0 : hi - lo, :].rearrange("p e c -> p (e c)")
+                out=y_half[:, g * GROUP_SLOTS : (g + 1) * GROUP_SLOTS], in_=bank[:].rearrange("p e c -> p (e c)")
             )
 
-        for g0 in (0, 2):
-            if g0 == 0:
-                for u, g in ((0, 0), (0, 1), (1, 0), (1, 1)):
-                    gather(u, g)
-            else:
-                for u, g in ((0, 2), (1, 2), (0, 3), (1, 3)):
-                    gather(u, g)
+        for e in range(ON_VECTOR, HALVED):
+            round_both(e, ON_VECTOR, nc.scalar.copy)
+        for e in range(HALVED, E):
+            round_half(0, e, nc.scalar.copy)
 
-        cast_whole(0, "vector")
-        cast_whole(1, "vector")
-        quantise_w2(0, 0, 2)
-        quantise_w2(1, 0, 2)
-        for e in range(2, 9):
-            cast_whole(e, "gpsimd")
-        cast_whole(9, "scalar")
-        interleave(0, "hs0")
-        interleave(1, "hs1")
-        interleave(2, "room9")
-        cast_whole(10, "scalar")
-        interleave(3, "room10")
-
-        for e in range(11, E):
-            cast_half(0, e)
+        for g in range(GROUPS):
+            gather(0, g)
+        gather(1, 0)
+        gather(1, 1)
+        for e in range(ON_VECTOR):
+            round_both(e, 0, nc.vector.tensor_copy)
+        for b in range(2):
+            quantise_w2(b, 0, ON_VECTOR)
+        interleave(0)
+        gather(1, 2)
+        interleave(1)
+        gather(1, 3)
         quantise_h(0)
-        quantise_w2(0, 2, 4)
-        experts(0, 0, 4)
+        interleave(2)
         quantise_h(1)
-        quantise_w2(0, 4, 8)
-        experts(0, 4, 8)
+        interleave(3)
         quantise_h(2)
+        quantise_h(3)
+
+        y = [sbuf([P, S], F32, "y0", "w2_half0_%d" % LAST), sbuf([P, S], F32, "y1")]
+        quantise_w2(0, 2, 4)
+        multiply(0, 0, y[0])
+        quantise_w2(0, 4, 8)
+        multiply(0, 1, y[0])
         quantise_w2(0, 8, 9)
         quantise_w2(0, 9, 11)
         quantise_w2(0, 11, 13)
-        experts(0, 8, 12)
-        quantise_h(3)
+        multiply(0, 2, y[0])
         quantise_w2(0, 13, 15)
         quantise_w2(0, 15, 16)
-        experts(0, 12, 16)
+        multiply(0, 3, y[0])
 
+        round_half(1, HALVED, nc.vector.tensor_copy)
+        code_runs.append((1, ON_VECTOR, E, sbuf([P, E - ON_VECTOR, P], U32, "late_codes1", "after_half0_codes")[:]))
+        for lo, hi, tag in ((DEFERRED, DEFERRED_CUT, "first_deferred"), (DEFERRED_CUT, E, "second_deferred")):
+            bf_runs.append((1, lo, hi, sbuf([P, hi - lo, P, 4], BF16, tag + "_bf", tag)[:]))
         quantise_w2(1, 2, 4)
         quantise_w2(1, 4, 8)
         quantise_w2(1, 8, 9)
-        quantise_w2(1, 9, 11)
-        cast_half(1, 11)
-        cast_half(1, 12)
-        quantise_w2(1, 11, 13)
-        cast_half(1, 13)
-        cast_half(1, 14)
-        quantise_w2(1, 13, 15)
-        cast_half(1, 15)
-        quantise_w2(1, 15, 16)
-        for g in range(4):
-            experts(1, 4 * g, 4 * g + 4)
+        quantise_w2(1, 9, 10)
+        for lo in range(DEFERRED, E, 2):
+            round_half(1, lo, nc.scalar.copy)
+            round_half(1, lo + 1, nc.scalar.copy)
+            quantise_w2(1, lo, lo + 2)
+        for g in range(GROUPS):
+            multiply(1, g, y[1])
 
-        pieces = []
-        for b in range(2):
-            lo = 0
-            for width in PIECES[b]:
-                pieces.append((b, lo, lo + width))
-                lo += width
-
+        pieces = [(b, sum(widths[:i]), sum(widths[: i + 1])) for b, widths in enumerate(PIECE_WIDTHS) for i in range(len(widths))]
         terms = {}
+        turned = sbuf([P, TURNED, T // 2], F32, "turned", "after_half0_codes")
 
-        def product(piece, r):
-            b, lo, hi = piece
-            tag = "room0_%d" % (E - 2) if (b, hi, r) == (0, T, 1) else "term%d_%d_%d" % (b, lo, r)
-            terms[(piece, r)] = keep.tile([P, hi - lo], F32, name="term%d_%d_%d" % (b, lo, r), tag=tag, align_bytes=64)
+        def product(i, r):
+            b, lo, hi = pieces[i]
+            tag = ("first_deferred", "second_deferred")[r] if (b, hi) == (0, T) else None
+            terms[(i, r)] = sbuf([P, hi - lo], F32, "term%d_%d" % (i, r), tag)
+            at = lo % (T // 2)
             nc.vector.tensor_tensor(
-                terms[(piece, r)][:], y[b][:].indirect(pos_lists[r][:, lo // 16 : hi // 16]), gates[lo // (T // 2)][:, r, lo % (T // 2) : lo % (T // 2) + hi - lo], MULT
+                terms[(i, r)][:],
+                y[b][:].indirect(pos_lists[r][:, lo // 16 : hi // 16]),
+                gates[lo // (T // 2)][:, r, at : at + hi - lo],
+                MULT,
             )
 
-        def finish(piece):
-            b, lo, hi = piece
-            nc.vector.tensor_tensor(res[:, b, lo:hi], terms[(piece, 0)][:], terms[(piece, 1)][:], ADD)
+        def store(i):
+            b, lo, hi = pieces[i]
             nc.sync.dma_start(out=out[b * P : (b + 1) * P, lo:hi], in_=res[:, b, lo:hi])
 
-        for i, piece in enumerate(pieces):
-            product(piece, 0)
-            if i > 0:
-                finish(pieces[i - 1])
-            product(piece, 1)
-        finish(pieces[-1])
+        def add_on_vector(i):
+            b, lo, hi = pieces[i]
+            nc.vector.tensor_tensor(res[:, b, lo:hi], terms[(i, 0)][:], terms[(i, 1)][:], ADD)
+            store(i)
+
+        def add_turned(i):
+            width = pieces[i][2] - pieces[i][1]
+            bank = psum.tile([P, width], F32, name="bank")
+            for c in range(0, width, P):
+                for r in range(2):
+                    nc.tensor.matmul(
+                        bank[:, c : c + P],
+                        terms[(i, r)][:, c : c + P],
+                        ident[:],
+                        start=(r == 0),
+                        stop=(r == 1),
+                        is_transpose=True,
+                    )
+            nc.scalar.copy(out=turned[:, i, 0:width], in_=bank[:])
+
+        def turn_back(i):
+            b, lo, hi = pieces[i]
+            bank = psum.tile([P, hi - lo], F32, name="bank")
+            for c in range(0, hi - lo, P):
+                nc.tensor.transpose(bank[:, c : c + P], turned[:, i, c : c + P], ident[:])
+            nc.scalar.copy(out=res[:, b, lo:hi], in_=bank[:])
+            store(i)
+
+        for i in range(len(pieces)):
+            product(i, 0)
+            if i > TURNED:
+                add_on_vector(i - 1)
+            product(i, 1)
+            if i < TURNED:
+                add_turned(i)
+            if 0 < i <= TURNED:
+                turn_back(i - 1)
+        add_on_vector(len(pieces) - 1)

@@ -25,16 +25,12 @@ GROUP = 4
 GROUP_SLOTS = GROUP * C
 GROUPS = E // GROUP
 
-ON_VECTOR = 2
-HALVED = 9
-DEFERRED = HALVED + 1
-SPLIT_LOAD = 14
+WHOLE = 4
 LAST = E - 1
-CODES_CUT = 13
-DEFERRED_CUT = 14
+BEFORE_Y = 7
 
-PIECE_WIDTHS = ((512, 512), (512, 256, 256))
-TURNED = 2
+PIECE_WIDTHS = ((512, 512), (256, 256, 256, 256))
+TURNED = 4
 
 
 def tile_moe_sup_lin_gelu_kernel(
@@ -43,10 +39,13 @@ def tile_moe_sup_lin_gelu_kernel(
     nc = tc.nc
     with ExitStack() as ctx:
         keep = ctx.enter_context(tc.tile_pool(name="keep", bufs=1))
-        psum = ctx.enter_context(tc.psum_pool(name="psum", bufs=BANKS))
+        psum = ctx.enter_context(tc.psum_pool(name="psum", bufs=1))
 
         def sbuf(shape, dtype, name, tag=None):
             return keep.tile(shape, dtype, name=name, tag=tag or name, align_bytes=64)
+
+        def psum_bank(shape, number):
+            return psum.tile(shape, F32, name="bank", tag="bank%d" % number)
 
         slot_list = keep.tile([P, S // 16], U16, name="slot_list")
         pos_lists = [keep.tile([P, T // 16], U16, name="pos_list%d" % r) for r in range(2)]
@@ -58,37 +57,34 @@ def tile_moe_sup_lin_gelu_kernel(
         w1_codes = sbuf([P, 4, P], U32, "w1_codes")
         w1_plane = sbuf([P, 4, P], U8, "w1_plane")
         h_pairs = [sbuf([P, T, 2], BF16, "h_pairs%d" % u) for u in range(2)]
-        picked = [sbuf([P, 2, GROUP_SLOTS, 2], BF16, "picked%d" % g) for g in range(GROUPS)]
-        hs_bf = [sbuf([P, GROUP_SLOTS, 4], BF16, "hs_bf%d" % g) for g in range(GROUPS)]
+        picked = [sbuf([P, 2, GROUP_SLOTS], U32, "picked%d" % g) for g in range(GROUPS)]
         hs_codes = sbuf([P, S], U32, "hs_codes")
         hs_plane = sbuf([P, S], U8, "hs_plane")
         w2_plane = sbuf([P, 2, E, P], U8, "w2_plane")
         gates = [sbuf([P, 2, T // 2], F32, "gates%d" % a) for a in range(2)]
-        res = sbuf([P, 2, T], F32, "res")
 
-        w2_whole = [sbuf([P, 4, N], F32, "w2_whole%d" % e) for e in range(SPLIT_LOAD)]
-        w2_raw = {(b, e): w2_whole[e][:, :, b * P : (b + 1) * P] for b in range(2) for e in range(SPLIT_LOAD)}
-        for b in range(2):
-            for e in range(SPLIT_LOAD, E):
-                w2_raw[(b, e)] = sbuf([P, 4, P], F32, "w2_half%d_%d" % (b, e))[:]
+        w2_whole = [sbuf([P, 4, N], F32, "w2_whole%d" % e) for e in range(WHOLE)]
+        w2_half = {(b, e): sbuf([P, 4, P], F32, "w2_half%d_%d" % (b, e)) for b in range(2) for e in range(WHOLE, E)}
 
-        both_bf = {
-            lo: sbuf([P, 2, hi - lo, P, 4], BF16, "both_bf%d" % lo) for lo, hi in ((0, ON_VECTOR), (ON_VECTOR, HALVED))
-        }
-        bf_runs = [(b, lo, lo + tile.shape[2], tile[:, b]) for lo, tile in both_bf.items() for b in range(2)]
-        bf_runs.append((0, HALVED, LAST, sbuf([P, LAST - HALVED, P, 4], BF16, "half0_bf")[:]))
-        bf_runs.append((0, LAST, E, sbuf([P, 1, P, 4], BF16, "last_bf", "after_half0_codes")[:]))
-        bf_runs.append((1, HALVED, DEFERRED, sbuf([P, 1, P, 4], BF16, "vector_half1_bf")[:]))
-        code_runs = [
-            (0, 0, HALVED, sbuf([P, HALVED, P], U32, "early_codes0")[:]),
-            (0, HALVED, CODES_CUT, sbuf([P, CODES_CUT - HALVED, P], U32, "late_codes0", "second_deferred")[:]),
-            (0, CODES_CUT, E, sbuf([P, E - CODES_CUT, P], U32, "last_codes0", "first_deferred")[:]),
-            (1, 0, ON_VECTOR, sbuf([P, ON_VECTOR, P], U32, "early_codes1")[:]),
-        ]
+        bf_runs = []
+        code_runs = []
 
         def experts_of(runs, b, lo, hi):
             first, view = [(first, view) for half, first, end, view in runs if half == b and first <= lo < end][0]
             return view[:, lo - first : hi - first]
+
+        def add_bf_run(b, lo, hi, tag=None):
+            tile = sbuf([P, (hi - lo) * P * 4], BF16, "bf%d_%d" % (b, lo), tag)
+            bf_runs.append((b, lo, hi, tile[:].rearrange("p (e n j) -> p e n j", n=P, j=4)))
+
+        def add_code_run(b, lo, hi, tag=None):
+            tile = sbuf([P, hi - lo, P], U32, "codes%d_%d" % (b, lo), tag)
+            code_runs.append((b, lo, hi, tile[:]))
+
+        def add_both_run(lo, hi, tag=None):
+            tile = sbuf([P, 2, hi - lo, P, 4], BF16, "both_bf%d" % lo, tag)
+            bf_runs.extend((b, lo, hi, tile[:, b]) for b in range(2))
+            return tile
 
         make_identity(nc, ident[:])
 
@@ -102,18 +98,20 @@ def tile_moe_sup_lin_gelu_kernel(
             )
         nc.sync.dma_start(out=x_codes[:].bitcast(I32), in_=x_words[0].rearrange("p t d -> p (t d)").bitcast(I32))
         w2_rows = [w2[e].rearrange("(p j) n -> p j n", j=4) for e in range(E)]
-        for e in range(SPLIT_LOAD):
+        for e in range(WHOLE):
             nc.sync.dma_start(out=w2_whole[e][:], in_=w2_rows[e])
             if e == 0:
                 nc.sync.dma_start(slot_list[:], offs)
-            if e == GROUP - 1:
-                nc.sync.dma_start(pos_lists[0][:], pos1)
-                nc.sync.dma_start(pos_lists[1][:], pos2)
         gate_rows = gate.rearrange("r p t -> p r t")
         for b in range(2):
-            for e in range(SPLIT_LOAD, E):
-                nc.sync.dma_start(out=w2_raw[(b, e)], in_=w2_rows[e][:, :, b * P : (b + 1) * P])
-            nc.sync.dma_start(out=gates[b][:], in_=gate_rows[:, :, b * T // 2 : (b + 1) * T // 2])
+            for e in range(WHOLE, E):
+                nc.sync.dma_start(out=w2_half[(b, e)][:], in_=w2_rows[e][:, :, b * P : (b + 1) * P])
+                if (b, e) == (1, WHOLE):
+                    nc.sync.dma_start(pos_lists[0][:], pos1)
+                    nc.sync.dma_start(pos_lists[1][:], pos2)
+                if b == 1 and e in (9, LAST):
+                    a = e // 10
+                    nc.sync.dma_start(out=gates[a][:], in_=gate_rows[:, :, a * T // 2 : (a + 1) * T // 2])
 
         for a in range(2):
             nc.vector.tensor_copy(
@@ -129,7 +127,7 @@ def tile_moe_sup_lin_gelu_kernel(
         for u in range(2):
             for lo in range(0, T, BANK_TOKENS):
                 tokens = slice(lo, lo + BANK_TOKENS)
-                bank = psum.tile([P, 2, BANK_TOKENS], F32, name="bank")
+                bank = psum_bank([P, 2, BANK_TOKENS], u * BANKS // 2 + lo // BANK_TOKENS)
                 for d in range(2):
                     nc.tensor.matmul_mx(
                         out=bank[:, d, :],
@@ -142,17 +140,20 @@ def tile_moe_sup_lin_gelu_kernel(
                     )
                 nc.scalar.activation(out=h_pairs[u][:, tokens, :], in_=bank[:].rearrange("p d t -> p t d"), func=GELU)
 
-        def round_both(e, first, copy):
+        def round_both(e, tile, at, copy):
             copy(
-                out=both_bf[first][:, :, e - first].rearrange("p b (c i) j -> p b c j i", i=4),
+                out=tile[:, :, at].rearrange("p b (c i) j -> p b c j i", i=4),
                 in_=w2_whole[e][:].rearrange("p j (b c i) -> p b c j i", b=2, i=4),
             )
 
         def round_half(b, e, copy):
             copy(
                 out=experts_of(bf_runs, b, e, e + 1)[:, 0].rearrange("p (c i) j -> p c j i", i=4),
-                in_=w2_raw[(b, e)].rearrange("p j (c i) -> p c j i", i=4),
+                in_=w2_half[(b, e)][:].rearrange("p j (c i) -> p c j i", i=4),
             )
+
+        def round_on_gpsimd(out, in_):
+            nc.gpsimd.tensor_scalar(out, in_, 1.0, 0.0, MULT, ADD)
 
         def quantise_w2(b, lo, hi):
             nc.vector.quantize_mx(
@@ -163,28 +164,26 @@ def tile_moe_sup_lin_gelu_kernel(
 
         def gather(u, g):
             nc.vector.tensor_copy(
-                picked[g][:, u].rearrange("p s d -> p (s d)").bitcast(U32),
+                picked[g][:, u],
                 h_pairs[u][:]
                 .rearrange("p t d -> p (t d)")
                 .bitcast(U32)
                 .indirect(slot_list[:, g * GROUP_SLOTS // 16 : (g + 1) * GROUP_SLOTS // 16]),
             )
 
+        hs_bf = {}
+
         def interleave(g):
-            nc.vector.tensor_copy(
-                out=hs_bf[g][:].rearrange("p s (u d) -> p s u d", u=2), in_=picked[g][:].rearrange("p u s d -> p s u d")
+            nc.scalar.copy(
+                out=hs_bf[g].bitcast(U32).rearrange("p (s u) -> p s u", u=2), in_=picked[g][:].rearrange("p u s -> p s u")
             )
 
         def quantise_h(g):
             slots = slice(g * GROUP_SLOTS, (g + 1) * GROUP_SLOTS)
-            nc.vector.quantize_mx(
-                out=hs_codes[:, slots].bitcast(FP8X4),
-                scales=hs_plane[:, slots],
-                in_=hs_bf[g][:].rearrange("p s j -> p (s j)"),
-            )
+            nc.vector.quantize_mx(out=hs_codes[:, slots].bitcast(FP8X4), scales=hs_plane[:, slots], in_=hs_bf[g])
 
         def multiply(b, g, y_half):
-            bank = psum.tile([P, GROUP, C], F32, name="bank")
+            bank = psum_bank([P, GROUP, C], b * GROUPS + g)
             for e in range(g * GROUP, (g + 1) * GROUP):
                 nc.tensor.matmul_mx(
                     out=bank[:, e % GROUP, :],
@@ -199,66 +198,77 @@ def tile_moe_sup_lin_gelu_kernel(
                 out=y_half[:, g * GROUP_SLOTS : (g + 1) * GROUP_SLOTS], in_=bank[:].rearrange("p e c -> p (e c)")
             )
 
-        for e in range(ON_VECTOR, HALVED):
-            round_both(e, ON_VECTOR, nc.scalar.copy)
-        for e in range(HALVED, E):
-            round_half(0, e, nc.scalar.copy)
+        for u in range(2):
+            for g in range(GROUPS):
+                gather(u, g)
 
-        for g in range(GROUPS):
-            gather(0, g)
-        gather(1, 0)
-        gather(1, 1)
-        for e in range(ON_VECTOR):
-            round_both(e, 0, nc.vector.tensor_copy)
+        first_bf = add_both_run(0, 1)
+        round_both(0, first_bf, 0, nc.vector.tensor_copy)
+        first_codes = sbuf([P, 2, 1, P], U32, "first_codes")
+        code_runs.extend((b, 0, 1, first_codes[:, b]) for b in range(2))
         for b in range(2):
-            quantise_w2(b, 0, ON_VECTOR)
-        interleave(0)
-        gather(1, 2)
-        interleave(1)
-        gather(1, 3)
-        quantise_h(0)
-        interleave(2)
-        quantise_h(1)
-        interleave(3)
-        quantise_h(2)
-        quantise_h(3)
+            quantise_w2(b, 0, 1)
+        gpsimd_bf = add_both_run(1, 3, "both_bf0")
+        for e in (1, 2):
+            round_on_gpsimd(gpsimd_bf[:, :, e - 1], w2_whole[e][:].rearrange("p j (b n) -> p b n j", b=2))
+        round_both(3, add_both_run(3, 4), 0, nc.scalar.copy)
+        for lo in range(WHOLE, E, GROUP):
+            add_bf_run(0, lo, lo + GROUP)
+        for e in range(WHOLE, E):
+            if e % 2 == 0 or e == LAST:
+                round_on_gpsimd(experts_of(bf_runs, 0, e, e + 1)[:, 0], w2_half[(0, e)][:].rearrange("p j n -> p n j"))
+            else:
+                round_half(0, e, nc.scalar.copy)
 
-        y = [sbuf([P, S], F32, "y0", "w2_half0_%d" % LAST), sbuf([P, S], F32, "y1")]
-        quantise_w2(0, 2, 4)
-        multiply(0, 0, y[0])
-        quantise_w2(0, 4, 8)
-        multiply(0, 1, y[0])
-        quantise_w2(0, 8, 9)
-        quantise_w2(0, 9, 11)
-        quantise_w2(0, 11, 13)
-        multiply(0, 2, y[0])
-        quantise_w2(0, 13, 15)
-        quantise_w2(0, 15, 16)
-        multiply(0, 3, y[0])
+        early_hs = sbuf([P, 2 * GROUP_SLOTS * 4], BF16, "early_hs", "w2_half0_10")
+        for g in range(GROUPS):
+            if g < 2:
+                hs_bf[g] = early_hs[:, g * GROUP_SLOTS * 4 : (g + 1) * GROUP_SLOTS * 4]
+            else:
+                hs_bf[g] = sbuf([P, GROUP_SLOTS * 4], BF16, "late_hs%d" % g, "picked%d" % (g - 2))[:]
+            interleave(g)
 
-        round_half(1, HALVED, nc.vector.tensor_copy)
-        code_runs.append((1, ON_VECTOR, E, sbuf([P, E - ON_VECTOR, P], U32, "late_codes1", "after_half0_codes")[:]))
-        for lo, hi, tag in ((DEFERRED, DEFERRED_CUT, "first_deferred"), (DEFERRED_CUT, E, "second_deferred")):
-            bf_runs.append((1, lo, hi, sbuf([P, hi - lo, P, 4], BF16, tag + "_bf", tag)[:]))
-        quantise_w2(1, 2, 4)
-        quantise_w2(1, 4, 8)
-        quantise_w2(1, 8, 9)
-        quantise_w2(1, 9, 10)
-        for lo in range(DEFERRED, E, 2):
-            round_half(1, lo, nc.scalar.copy)
-            round_half(1, lo + 1, nc.scalar.copy)
-            quantise_w2(1, lo, lo + 2)
+        add_code_run(0, 1, WHOLE, "w2_half0_6")
+        add_code_run(0, WHOLE, E)
+        quantise_w2(0, 1, 3)
+        quantise_w2(0, 3, 4)
+        for g in range(GROUPS):
+            if g > 0:
+                quantise_w2(0, g * GROUP, (g + 1) * GROUP)
+            quantise_h(g)
+
+        add_bf_run(1, 4, 6)
+        add_bf_run(1, 6, 8)
+        for lo in range(2 * GROUP, E, GROUP):
+            add_bf_run(1, lo, lo + GROUP)
+        for e in range(WHOLE, BEFORE_Y):
+            round_half(1, e, nc.scalar.copy)
+        y = [sbuf([P, S], F32, "y0", "w2_half1_%d" % (BEFORE_Y - 2)), sbuf([P, S], F32, "y1")]
+        for g in range(GROUPS):
+            multiply(0, g, y[0])
+
+        add_code_run(1, 1, 6, "picked1")
+        add_code_run(1, 6, E)
+        quantise_w2(1, 1, 3)
+        quantise_w2(1, 3, 4)
+        quantise_w2(1, 4, 6)
+        for e in range(BEFORE_Y, E):
+            round_half(1, e, nc.scalar.copy)
+        quantise_w2(1, 6, 8)
+        quantise_w2(1, 8, 12)
+        quantise_w2(1, 12, 16)
         for g in range(GROUPS):
             multiply(1, g, y[1])
 
         pieces = [(b, sum(widths[:i]), sum(widths[: i + 1])) for b, widths in enumerate(PIECE_WIDTHS) for i in range(len(widths))]
         terms = {}
-        turned = sbuf([P, TURNED, T // 2], F32, "turned", "after_half0_codes")
+        turned = [sbuf([P, T // 2], F32, "turned%d" % i, "w2_whole%d" % i) for i in range(TURNED)]
+        res = {}
+        term_tags = {(0, 1): "w2_half1_8", (1, 0): "w2_half1_12", (1, 1): "w2_half1_15"}
 
         def product(i, r):
             b, lo, hi = pieces[i]
-            tag = ("first_deferred", "second_deferred")[r] if (b, hi) == (0, T) else None
-            terms[(i, r)] = sbuf([P, hi - lo], F32, "term%d_%d" % (i, r), tag)
+            terms[(i, r)] = sbuf([P, hi - lo], F32, "term%d_%d" % (i, r), term_tags.get((i, r)))
             at = lo % (T // 2)
             nc.vector.tensor_tensor(
                 terms[(i, r)][:],
@@ -269,16 +279,17 @@ def tile_moe_sup_lin_gelu_kernel(
 
         def store(i):
             b, lo, hi = pieces[i]
-            nc.sync.dma_start(out=out[b * P : (b + 1) * P, lo:hi], in_=res[:, b, lo:hi])
+            nc.sync.dma_start(out=out[b * P : (b + 1) * P, lo:hi], in_=res[i])
 
         def add_on_vector(i):
             b, lo, hi = pieces[i]
-            nc.vector.tensor_tensor(res[:, b, lo:hi], terms[(i, 0)][:], terms[(i, 1)][:], ADD)
+            res[i] = last_res[:, lo - T // 2 : hi - T // 2]
+            nc.vector.tensor_tensor(res[i], terms[(i, 0)][:], terms[(i, 1)][:], ADD)
             store(i)
 
         def add_turned(i):
             width = pieces[i][2] - pieces[i][1]
-            bank = psum.tile([P, width], F32, name="bank")
+            bank = psum_bank([P, width], i)
             for c in range(0, width, P):
                 for r in range(2):
                     nc.tensor.matmul(
@@ -289,23 +300,28 @@ def tile_moe_sup_lin_gelu_kernel(
                         stop=(r == 1),
                         is_transpose=True,
                     )
-            nc.scalar.copy(out=turned[:, i, 0:width], in_=bank[:])
+            nc.scalar.copy(out=turned[i][:, 0:width], in_=bank[:])
 
         def turn_back(i):
             b, lo, hi = pieces[i]
-            bank = psum.tile([P, hi - lo], F32, name="bank")
+            bank = psum_bank([P, hi - lo], (i + 2) % TURNED)
             for c in range(0, hi - lo, P):
-                nc.tensor.transpose(bank[:, c : c + P], turned[:, i, c : c + P], ident[:])
-            nc.scalar.copy(out=res[:, b, lo:hi], in_=bank[:])
+                nc.tensor.transpose(bank[:, c : c + P], turned[i][:, c : c + P], ident[:])
+            res[i] = sbuf([P, hi - lo], F32, "res%d" % i)[:]
+            nc.scalar.copy(out=res[i], in_=bank[:])
             store(i)
 
-        for i in range(len(pieces)):
+        for i in range(TURNED):
+            product(i, 0)
+            product(i, 1)
+            add_turned(i)
+            if i % 2 == 1:
+                turn_back(i - 1)
+                turn_back(i)
+        last_res = sbuf([P, T // 2], F32, "last_res", "w2_whole%d" % (TURNED - 1))
+        for i in range(TURNED, len(pieces)):
             product(i, 0)
             if i > TURNED:
                 add_on_vector(i - 1)
             product(i, 1)
-            if i < TURNED:
-                add_turned(i)
-            if 0 < i <= TURNED:
-                turn_back(i - 1)
         add_on_vector(len(pieces) - 1)

@@ -25,9 +25,11 @@ GROUP = 4
 GROUP_SLOTS = GROUP * C
 GROUPS = E // GROUP
 
-WHOLE = 4
+EARLY = 9
+EARLY_ON_SCALAR = (3, 5, 6)
+SPLIT_LOAD = 14
 LAST = E - 1
-BEFORE_Y = 7
+LATE_RUNS = ((EARLY, 13), (13, LAST), (LAST, E))
 
 PIECE_WIDTHS = ((512, 512), (256, 256, 256, 256))
 TURNED = 4
@@ -63,8 +65,11 @@ def tile_moe_sup_lin_gelu_kernel(
         w2_plane = sbuf([P, 2, E, P], U8, "w2_plane")
         gates = [sbuf([P, 2, T // 2], F32, "gates%d" % a) for a in range(2)]
 
-        w2_whole = [sbuf([P, 4, N], F32, "w2_whole%d" % e) for e in range(WHOLE)]
-        w2_half = {(b, e): sbuf([P, 4, P], F32, "w2_half%d_%d" % (b, e)) for b in range(2) for e in range(WHOLE, E)}
+        w2_whole = [sbuf([P, 4, N], F32, "w2_whole%d" % e) for e in range(SPLIT_LOAD)]
+        w2_raw = {(b, e): w2_whole[e][:, :, b * P : (b + 1) * P] for b in range(2) for e in range(SPLIT_LOAD)}
+        for b in range(2):
+            for e in range(SPLIT_LOAD, E):
+                w2_raw[(b, e)] = sbuf([P, 4, P], F32, "w2_half%d_%d" % (b, e))[:]
 
         bf_runs = []
         code_runs = []
@@ -98,20 +103,18 @@ def tile_moe_sup_lin_gelu_kernel(
             )
         nc.sync.dma_start(out=x_codes[:].bitcast(I32), in_=x_words[0].rearrange("p t d -> p (t d)").bitcast(I32))
         w2_rows = [w2[e].rearrange("(p j) n -> p j n", j=4) for e in range(E)]
-        for e in range(WHOLE):
+        for e in range(SPLIT_LOAD):
             nc.sync.dma_start(out=w2_whole[e][:], in_=w2_rows[e])
             if e == 0:
                 nc.sync.dma_start(slot_list[:], offs)
+            if e == EARLY:
+                nc.sync.dma_start(pos_lists[0][:], pos1)
+                nc.sync.dma_start(pos_lists[1][:], pos2)
         gate_rows = gate.rearrange("r p t -> p r t")
         for b in range(2):
-            for e in range(WHOLE, E):
-                nc.sync.dma_start(out=w2_half[(b, e)][:], in_=w2_rows[e][:, :, b * P : (b + 1) * P])
-                if (b, e) == (1, WHOLE):
-                    nc.sync.dma_start(pos_lists[0][:], pos1)
-                    nc.sync.dma_start(pos_lists[1][:], pos2)
-                if b == 1 and e in (9, LAST):
-                    a = e // 10
-                    nc.sync.dma_start(out=gates[a][:], in_=gate_rows[:, :, a * T // 2 : (a + 1) * T // 2])
+            for e in range(SPLIT_LOAD, E):
+                nc.sync.dma_start(out=w2_raw[(b, e)], in_=w2_rows[e][:, :, b * P : (b + 1) * P])
+            nc.sync.dma_start(out=gates[b][:], in_=gate_rows[:, :, b * T // 2 : (b + 1) * T // 2])
 
         for a in range(2):
             nc.vector.tensor_copy(
@@ -149,11 +152,8 @@ def tile_moe_sup_lin_gelu_kernel(
         def round_half(b, e, copy):
             copy(
                 out=experts_of(bf_runs, b, e, e + 1)[:, 0].rearrange("p (c i) j -> p c j i", i=4),
-                in_=w2_half[(b, e)][:].rearrange("p j (c i) -> p c j i", i=4),
+                in_=w2_raw[(b, e)].rearrange("p j (c i) -> p c j i", i=4),
             )
-
-        def round_on_gpsimd(out, in_):
-            nc.gpsimd.tensor_scalar(out, in_, 1.0, 0.0, MULT, ADD)
 
         def quantise_w2(b, lo, hi):
             nc.vector.quantize_mx(
@@ -174,9 +174,16 @@ def tile_moe_sup_lin_gelu_kernel(
         hs_bf = {}
 
         def interleave(g):
-            nc.scalar.copy(
-                out=hs_bf[g].bitcast(U32).rearrange("p (s u) -> p s u", u=2), in_=picked[g][:].rearrange("p u s -> p s u")
-            )
+            if g < GROUPS - 1:
+                nc.scalar.copy(
+                    out=hs_bf[g].bitcast(U32).rearrange("p (s u) -> p s u", u=2),
+                    in_=picked[g][:].rearrange("p u s -> p s u"),
+                )
+            else:
+                nc.vector.tensor_copy(
+                    out=hs_bf[g].rearrange("p (s u d) -> p s u d", u=2, d=2),
+                    in_=picked[g][:].bitcast(BF16).rearrange("p u (s d) -> p s u d", d=2),
+                )
 
         def quantise_h(g):
             slots = slice(g * GROUP_SLOTS, (g + 1) * GROUP_SLOTS)
@@ -208,55 +215,61 @@ def tile_moe_sup_lin_gelu_kernel(
         code_runs.extend((b, 0, 1, first_codes[:, b]) for b in range(2))
         for b in range(2):
             quantise_w2(b, 0, 1)
-        gpsimd_bf = add_both_run(1, 3, "both_bf0")
-        for e in (1, 2):
-            round_on_gpsimd(gpsimd_bf[:, :, e - 1], w2_whole[e][:].rearrange("p j (b n) -> p b n j", b=2))
-        round_both(3, add_both_run(3, 4), 0, nc.scalar.copy)
-        for lo in range(WHOLE, E, GROUP):
-            add_bf_run(0, lo, lo + GROUP)
-        for e in range(WHOLE, E):
-            if e % 2 == 0 or e == LAST:
-                round_on_gpsimd(experts_of(bf_runs, 0, e, e + 1)[:, 0], w2_half[(0, e)][:].rearrange("p j n -> p n j"))
-            else:
-                round_half(0, e, nc.scalar.copy)
+        for b in range(2):
+            for lo in range(1, EARLY, GROUP):
+                add_bf_run(b, lo, lo + GROUP, "both_bf0" if (b, lo) == (0, 1) else None)
+        for lo, hi in LATE_RUNS:
+            add_bf_run(0, lo, hi)
+        add_bf_run(1, EARLY, EARLY + 1)
 
-        early_hs = sbuf([P, 2 * GROUP_SLOTS * 4], BF16, "early_hs", "w2_half0_10")
+        def round_half_on_gpsimd(b, e):
+            nc.gpsimd.tensor_scalar(
+                experts_of(bf_runs, b, e, e + 1)[:, 0], w2_raw[(b, e)].rearrange("p j n -> p n j"), 1.0, 0.0, MULT, ADD
+            )
+
+        for e in range(1, EARLY):
+            for b in range(2):
+                if e in EARLY_ON_SCALAR:
+                    round_half(b, e, nc.scalar.copy)
+                else:
+                    round_half_on_gpsimd(b, e)
+
+        early_hs = sbuf([P, 2 * GROUP_SLOTS * 4], BF16, "early_hs", "w2_whole%d" % EARLY_ON_SCALAR[-1])
         for g in range(GROUPS):
             if g < 2:
                 hs_bf[g] = early_hs[:, g * GROUP_SLOTS * 4 : (g + 1) * GROUP_SLOTS * 4]
             else:
                 hs_bf[g] = sbuf([P, GROUP_SLOTS * 4], BF16, "late_hs%d" % g, "picked%d" % (g - 2))[:]
             interleave(g)
+        for e in range(EARLY, E):
+            round_half(0, e, nc.scalar.copy)
+        round_half(1, EARLY, nc.scalar.copy)
 
-        add_code_run(0, 1, WHOLE, "w2_half0_6")
-        add_code_run(0, WHOLE, E)
-        quantise_w2(0, 1, 3)
-        quantise_w2(0, 3, 4)
-        for g in range(GROUPS):
-            if g > 0:
-                quantise_w2(0, g * GROUP, (g + 1) * GROUP)
-            quantise_h(g)
-
-        add_bf_run(1, 4, 6)
-        add_bf_run(1, 6, 8)
-        for lo in range(2 * GROUP, E, GROUP):
-            add_bf_run(1, lo, lo + GROUP)
-        for e in range(WHOLE, BEFORE_Y):
-            round_half(1, e, nc.scalar.copy)
-        y = [sbuf([P, S], F32, "y0", "w2_half1_%d" % (BEFORE_Y - 2)), sbuf([P, S], F32, "y1")]
+        add_code_run(0, 1, EARLY)
+        add_code_run(0, EARLY, E)
+        quantise_w2(0, 1, 5)
+        quantise_h(0)
+        quantise_h(1)
+        quantise_w2(0, 5, EARLY)
+        quantise_h(2)
+        quantise_h(3)
+        for lo, hi in LATE_RUNS:
+            quantise_w2(0, lo, hi)
+        y = [sbuf([P, S], F32, "y0", "w2_half0_%d" % SPLIT_LOAD), sbuf([P, S], F32, "y1")]
         for g in range(GROUPS):
             multiply(0, g, y[0])
 
-        add_code_run(1, 1, 6, "picked1")
-        add_code_run(1, 6, E)
-        quantise_w2(1, 1, 3)
-        quantise_w2(1, 3, 4)
-        quantise_w2(1, 4, 6)
-        for e in range(BEFORE_Y, E):
+        add_code_run(1, 1, EARLY + 1, "bf0_%d" % LAST)
+        add_code_run(1, EARLY + 1, E)
+        quantise_w2(1, 1, 5)
+        quantise_w2(1, 5, EARLY)
+        quantise_w2(1, EARLY, EARLY + 1)
+        add_bf_run(1, EARLY + 1, SPLIT_LOAD, "codes0_%d" % EARLY)
+        add_bf_run(1, SPLIT_LOAD, E)
+        for e in range(EARLY + 1, E):
             round_half(1, e, nc.scalar.copy)
-        quantise_w2(1, 6, 8)
-        quantise_w2(1, 8, 12)
-        quantise_w2(1, 12, 16)
+        quantise_w2(1, EARLY + 1, SPLIT_LOAD)
+        quantise_w2(1, SPLIT_LOAD, E)
         for g in range(GROUPS):
             multiply(1, g, y[1])
 
@@ -264,7 +277,7 @@ def tile_moe_sup_lin_gelu_kernel(
         terms = {}
         turned = [sbuf([P, T // 2], F32, "turned%d" % i, "w2_whole%d" % i) for i in range(TURNED)]
         res = {}
-        term_tags = {(0, 1): "w2_half1_8", (1, 0): "w2_half1_12", (1, 1): "w2_half1_15"}
+        term_tags = {(1, 0): "w2_half1_14", (1, 1): "w2_half1_15"}
 
         def product(i, r):
             b, lo, hi = pieces[i]

@@ -31,8 +31,8 @@ SPLIT_LOAD = 14
 LAST = E - 1
 LATE_RUNS = ((EARLY, 13), (13, LAST), (LAST, E))
 
-PIECE_WIDTHS = ((512, 512), (256, 256, 256, 256))
-TURNED = 4
+PIECE_WIDTHS = ((512, 512), (512, 256, 256))
+TURNED = 2
 
 
 def tile_moe_sup_lin_gelu_kernel(
@@ -296,7 +296,7 @@ def tile_moe_sup_lin_gelu_kernel(
 
         def add_on_vector(i):
             b, lo, hi = pieces[i]
-            res[i] = last_res[:, lo - T // 2 : hi - T // 2]
+            res[i] = late_res[:, lo:hi] if i == TURNED else last_res[:, lo - T // 2 : hi - T // 2]
             nc.vector.tensor_tensor(res[i], terms[(i, 0)][:], terms[(i, 1)][:], ADD)
             store(i)
 
@@ -317,7 +317,7 @@ def tile_moe_sup_lin_gelu_kernel(
 
         def turn_back(i):
             b, lo, hi = pieces[i]
-            bank = psum_bank([P, hi - lo], (i + 2) % TURNED)
+            bank = psum_bank([P, hi - lo], TURNED + i)
             for c in range(0, hi - lo, P):
                 nc.tensor.transpose(bank[:, c : c + P], turned[i][:, c : c + P], ident[:])
             res[i] = sbuf([P, hi - lo], F32, "res%d" % i)[:]
@@ -331,7 +331,8 @@ def tile_moe_sup_lin_gelu_kernel(
             if i % 2 == 1:
                 turn_back(i - 1)
                 turn_back(i)
-        last_res = sbuf([P, T // 2], F32, "last_res", "w2_whole%d" % (TURNED - 1))
+        late_res = sbuf([P, T // 2], F32, "late_res", "w2_whole0")
+        last_res = sbuf([P, T // 2], F32, "last_res", "w2_whole1")
         for i in range(TURNED, len(pieces)):
             product(i, 0)
             if i > TURNED:

@@ -24,12 +24,19 @@ BANK_TOKENS = 256
 GROUP = 4
 GROUP_SLOTS = GROUP * C
 GROUPS = E // GROUP
+GATHER_EDGES = (0, 384, 1024, 1536, 2048)
 
-EARLY = 9
-EARLY_ON_SCALAR = (3, 5, 6)
+HEAD = 1
+EARLY = 10
+EARLY_ON_SCALAR = (3, 6)
 SPLIT_LOAD = 14
 LAST = E - 1
-LATE_RUNS = ((EARLY, 13), (13, LAST), (LAST, E))
+RUNS = (
+    ((0, 1), (1, 5), (5, 9), (9, 13), (13, 15), (15, 16)),
+    ((0, 1), (1, 9), (9, 11), (11, 15), (15, 16)),
+)
+BANK_RUNS = (((0, 4), (4, 8), (8, 12), (12, 15), (15, 16)), ((0, 4), (4, 8), (8, 12), (12, 16)))
+Y_BANKS = ((0, 1, 2, 3, 7), (4, 5, 6, 7))
 
 PIECE_WIDTHS = ((512, 512), (512, 256, 256))
 TURNED = 2
@@ -52,62 +59,53 @@ def tile_moe_sup_lin_gelu_kernel(
         slot_list = keep.tile([P, S // 16], U16, name="slot_list")
         pos_lists = [keep.tile([P, T // 16], U16, name="pos_list%d" % r) for r in range(2)]
         ident = sbuf([P, P], F32, "ident")
-        x_codes = sbuf([P, T], U32, "x_codes")
+        x_codes = [sbuf([P, BANK_TOKENS], U32, "x_first"), sbuf([P, T - BANK_TOKENS], U32, "x_rest")]
         x_plane = sbuf([P, T], U8, "x_plane")
         w1_raw = [sbuf([P, 4, H // 2], F32, "w1_raw%d" % a) for a in range(2)]
         w1_bf = sbuf([P, 4, P, 4], BF16, "w1_bf")
         w1_codes = sbuf([P, 4, P], U32, "w1_codes")
         w1_plane = sbuf([P, 4, P], U8, "w1_plane")
         h_pairs = [sbuf([P, T, 2], BF16, "h_pairs%d" % u) for u in range(2)]
-        picked = [sbuf([P, 2, GROUP_SLOTS], U32, "picked%d" % g) for g in range(GROUPS)]
-        hs_codes = sbuf([P, S], U32, "hs_codes")
+        picked = {}
         hs_plane = sbuf([P, S], U8, "hs_plane")
-        w2_plane = sbuf([P, 2, E, P], U8, "w2_plane")
         gates = [sbuf([P, 2, T // 2], F32, "gates%d" % a) for a in range(2)]
 
-        w2_whole = [sbuf([P, 4, N], F32, "w2_whole%d" % e) for e in range(SPLIT_LOAD)]
+        w2_whole = [sbuf([P, 4, N], F32, "w2_whole%d" % e)[:] for e in range(SPLIT_LOAD)]
         w2_raw = {(b, e): w2_whole[e][:, :, b * P : (b + 1) * P] for b in range(2) for e in range(SPLIT_LOAD)}
-        for b in range(2):
-            for e in range(SPLIT_LOAD, E):
-                w2_raw[(b, e)] = sbuf([P, 4, P], F32, "w2_half%d_%d" % (b, e))[:]
+        for e in range(SPLIT_LOAD, E):
+            w2_raw[(0, e)] = sbuf([P, 4, P], F32, "w2_half0_%d" % e)[:]
+            w2_raw[(1, e)] = sbuf([P, 4, P], F32, "w2_half1_%d" % e)[:]
 
-        bf_runs = []
-        code_runs = []
+        bf = {}
+        codes = {}
+        planes = {}
 
-        def experts_of(runs, b, lo, hi):
-            first, view = [(first, view) for half, first, end, view in runs if half == b and first <= lo < end][0]
-            return view[:, lo - first : hi - first]
+        def run_of(b, e):
+            return [run for run in RUNS[b] if run[0] <= e < run[1]][0]
 
-        def add_bf_run(b, lo, hi, tag=None):
-            tile = sbuf([P, (hi - lo) * P * 4], BF16, "bf%d_%d" % (b, lo), tag)
-            bf_runs.append((b, lo, hi, tile[:].rearrange("p (e n j) -> p e n j", n=P, j=4)))
-
-        def add_code_run(b, lo, hi, tag=None):
-            tile = sbuf([P, hi - lo, P], U32, "codes%d_%d" % (b, lo), tag)
-            code_runs.append((b, lo, hi, tile[:]))
-
-        def add_both_run(lo, hi, tag=None):
-            tile = sbuf([P, 2, hi - lo, P, 4], BF16, "both_bf%d" % lo, tag)
-            bf_runs.extend((b, lo, hi, tile[:, b]) for b in range(2))
-            return tile
+        def add_bf(b, lo, tag=None):
+            hi = run_of(b, lo)[1]
+            bf[(b, lo)] = sbuf([P, (hi - lo) * P * 4], BF16, "bf%d_%d" % (b, lo), tag)
 
         make_identity(nc, ident[:])
 
         w1_rows = w1.rearrange("(p j) c -> p j c", j=4)
         for a in range(2):
             nc.sync.dma_start(out=w1_raw[a][:], in_=w1_rows[:, :, a * H // 2 : (a + 1) * H // 2])
+        x_rows = x_words[0].rearrange("p t d -> p (t d)").bitcast(I32)
+        nc.sync.dma_start(out=x_codes[0][:].bitcast(I32), in_=x_rows[:, 0:BANK_TOKENS])
         nc.vector.memset(x_plane[:].bitcast(I32), 0)
         for q in range(4):
             nc.sync.dma_start(
                 out=x_plane[32 * q : 32 * q + 4, :].bitcast(I32), in_=x_scales[0, 4 * q : 4 * q + 4, :].bitcast(I32)
             )
-        nc.sync.dma_start(out=x_codes[:].bitcast(I32), in_=x_words[0].rearrange("p t d -> p (t d)").bitcast(I32))
+        nc.sync.dma_start(out=x_codes[1][:].bitcast(I32), in_=x_rows[:, BANK_TOKENS:T])
         w2_rows = [w2[e].rearrange("(p j) n -> p j n", j=4) for e in range(E)]
         for e in range(SPLIT_LOAD):
-            nc.sync.dma_start(out=w2_whole[e][:], in_=w2_rows[e])
+            nc.sync.dma_start(out=w2_whole[e], in_=w2_rows[e])
             if e == 0:
                 nc.sync.dma_start(slot_list[:], offs)
-            if e == EARLY:
+            if e == EARLY - 1:
                 nc.sync.dma_start(pos_lists[0][:], pos1)
                 nc.sync.dma_start(pos_lists[1][:], pos2)
         gate_rows = gate.rearrange("r p t -> p r t")
@@ -116,17 +114,25 @@ def tile_moe_sup_lin_gelu_kernel(
                 nc.sync.dma_start(out=w2_raw[(b, e)], in_=w2_rows[e][:, :, b * P : (b + 1) * P])
             nc.sync.dma_start(out=gates[b][:], in_=gate_rows[:, :, b * T // 2 : (b + 1) * T // 2])
 
-        for a in range(2):
+        def round_w1(a, lo, hi):
             nc.vector.tensor_copy(
-                out=w1_bf[:].rearrange("p t m j -> p m t j")[:, a * P // 2 : (a + 1) * P // 2],
-                in_=w1_raw[a][:].rearrange("p j (m t) -> p m t j", t=4),
+                out=w1_bf[:].rearrange("p t m j -> p m j t")[:, a * P // 2 : (a + 1) * P // 2, :, lo:hi],
+                in_=w1_raw[a][:].rearrange("p j (m t) -> p m j t", t=4)[:, :, :, lo:hi],
             )
-        for u in range(2):
+
+        def quantise_w1(lo, hi):
             nc.vector.quantize_mx(
-                out=w1_codes[:, 2 * u : 2 * u + 2].rearrange("p t m -> p (t m)").bitcast(FP8X4),
-                scales=w1_plane[:, 2 * u : 2 * u + 2].rearrange("p t m -> p (t m)"),
-                in_=w1_bf[:, 2 * u : 2 * u + 2].rearrange("p t m j -> p (t m j)"),
+                out=w1_codes[:, lo:hi].rearrange("p t m -> p (t m)").bitcast(FP8X4),
+                scales=w1_plane[:, lo:hi].rearrange("p t m -> p (t m)"),
+                in_=w1_bf[:, lo:hi].rearrange("p t m j -> p (t m j)"),
             )
+
+        round_w1(0, 0, 4)
+        round_w1(1, 0, 2)
+        quantise_w1(0, 1)
+        quantise_w1(1, 2)
+        round_w1(1, 2, 4)
+        quantise_w1(2, 4)
         for u in range(2):
             for lo in range(0, T, BANK_TOKENS):
                 tokens = slice(lo, lo + BANK_TOKENS)
@@ -136,31 +142,28 @@ def tile_moe_sup_lin_gelu_kernel(
                         out=bank[:, d, :],
                         lhsT=w1_codes[:, 2 * u + d, :].bitcast(FP8X4),
                         lhsT_scale=w1_plane[:, 2 * u + d, :],
-                        rhs=x_codes[:, tokens].bitcast(FP8X4),
+                        rhs=(x_codes[0][:] if lo == 0 else x_codes[1][:, lo - BANK_TOKENS : lo]).bitcast(FP8X4),
                         rhs_scale=x_plane[:, tokens],
                         start=True,
                         stop=True,
                     )
                 nc.scalar.activation(out=h_pairs[u][:, tokens, :], in_=bank[:].rearrange("p d t -> p t d"), func=GELU)
 
-        def round_both(e, tile, at, copy):
-            copy(
-                out=tile[:, :, at].rearrange("p b (c i) j -> p b c j i", i=4),
-                in_=w2_whole[e][:].rearrange("p j (b c i) -> p b c j i", b=2, i=4),
-            )
+        def bf_of(b, e):
+            lo = run_of(b, e)[0]
+            return bf[(b, lo)][:, (e - lo) * P * 4 : (e - lo + 1) * P * 4].rearrange("p (n j) -> p n j", j=4)
 
         def round_half(b, e, copy):
             copy(
-                out=experts_of(bf_runs, b, e, e + 1)[:, 0].rearrange("p (c i) j -> p c j i", i=4),
-                in_=w2_raw[(b, e)].rearrange("p j (c i) -> p c j i", i=4),
+                out=bf_of(b, e).rearrange("p (c i) j -> p c j i", i=2),
+                in_=w2_raw[(b, e)].rearrange("p j (c i) -> p c j i", i=2),
             )
 
-        def quantise_w2(b, lo, hi):
-            nc.vector.quantize_mx(
-                out=experts_of(code_runs, b, lo, hi).rearrange("p e n -> p (e n)").bitcast(FP8X4),
-                scales=w2_plane[:, b, lo:hi].rearrange("p e n -> p (e n)"),
-                in_=experts_of(bf_runs, b, lo, hi).rearrange("p e n j -> p (e n j)"),
-            )
+        def quantise_w2(b, lo, tag=None):
+            hi = run_of(b, lo)[1]
+            codes[(b, lo)] = sbuf([P, (hi - lo) * P], U32, "codes%d_%d" % (b, lo), tag)
+            planes[(b, lo)] = sbuf([P, (hi - lo) * P], U8, "plane%d_%d" % (b, lo))
+            nc.vector.quantize_mx(out=codes[(b, lo)][:].bitcast(FP8X4), scales=planes[(b, lo)][:], in_=bf[(b, lo)][:])
 
         def gather(u, g):
             nc.vector.tensor_copy(
@@ -168,116 +171,119 @@ def tile_moe_sup_lin_gelu_kernel(
                 h_pairs[u][:]
                 .rearrange("p t d -> p (t d)")
                 .bitcast(U32)
-                .indirect(slot_list[:, g * GROUP_SLOTS // 16 : (g + 1) * GROUP_SLOTS // 16]),
+                .indirect(slot_list[:, GATHER_EDGES[g] // 16 : GATHER_EDGES[g + 1] // 16]),
             )
 
         hs_bf = {}
 
-        def interleave(g):
-            if g < GROUPS - 1:
-                nc.scalar.copy(
-                    out=hs_bf[g].bitcast(U32).rearrange("p (s u) -> p s u", u=2),
-                    in_=picked[g][:].rearrange("p u s -> p s u"),
-                )
-            else:
-                nc.vector.tensor_copy(
-                    out=hs_bf[g].rearrange("p (s u d) -> p s u d", u=2, d=2),
-                    in_=picked[g][:].bitcast(BF16).rearrange("p u (s d) -> p s u d", d=2),
-                )
+        def interleave(g, words):
+            nc.scalar.copy(out=words.rearrange("p (s u) -> p s u", u=2), in_=picked[g][:].rearrange("p u s -> p s u"))
 
         def quantise_h(g):
             slots = slice(g * GROUP_SLOTS, (g + 1) * GROUP_SLOTS)
             nc.vector.quantize_mx(out=hs_codes[:, slots].bitcast(FP8X4), scales=hs_plane[:, slots], in_=hs_bf[g])
 
-        def multiply(b, g, y_half):
-            bank = psum_bank([P, GROUP, C], b * GROUPS + g)
-            for e in range(g * GROUP, (g + 1) * GROUP):
+        def multiply(b, i):
+            lo, hi = BANK_RUNS[b][i]
+            bank = psum_bank([P, hi - lo, C], Y_BANKS[b][i])
+            for e in range(lo, hi):
+                first = run_of(b, e)[0]
+                columns = slice((e - first) * P, (e - first + 1) * P)
                 nc.tensor.matmul_mx(
-                    out=bank[:, e % GROUP, :],
-                    lhsT=experts_of(code_runs, b, e, e + 1)[:, 0].bitcast(FP8X4),
-                    lhsT_scale=w2_plane[:, b, e],
+                    out=bank[:, e - lo, :],
+                    lhsT=codes[(b, first)][:, columns].bitcast(FP8X4),
+                    lhsT_scale=planes[(b, first)][:, columns],
                     rhs=hs_codes[:, e * C : (e + 1) * C].bitcast(FP8X4),
                     rhs_scale=hs_plane[:, e * C : (e + 1) * C],
                     start=True,
                     stop=True,
                 )
-            nc.scalar.copy(
-                out=y_half[:, g * GROUP_SLOTS : (g + 1) * GROUP_SLOTS], in_=bank[:].rearrange("p e c -> p (e c)")
-            )
+            nc.scalar.copy(out=y[b][:, lo * C : hi * C], in_=bank[:].rearrange("p e c -> p (e c)"))
 
+        def add_picked(g, tag=None):
+            picked[g] = sbuf([P, 2, GATHER_EDGES[g + 1] - GATHER_EDGES[g]], U32, "picked%d" % g, tag)
+
+        for g in range(2):
+            add_picked(g)
         for u in range(2):
-            for g in range(GROUPS):
+            for g in range(2):
                 gather(u, g)
 
-        first_bf = add_both_run(0, 1)
-        round_both(0, first_bf, 0, nc.vector.tensor_copy)
-        first_codes = sbuf([P, 2, 1, P], U32, "first_codes")
-        code_runs.extend((b, 0, 1, first_codes[:, b]) for b in range(2))
+        for lo, hi in RUNS[0]:
+            if lo != 1:
+                add_bf(0, lo)
+        add_bf(1, 0)
         for b in range(2):
-            quantise_w2(b, 0, 1)
+            round_half(b, 0, nc.vector.tensor_copy)
         for b in range(2):
-            for lo in range(1, EARLY, GROUP):
-                add_bf_run(b, lo, lo + GROUP, "both_bf0" if (b, lo) == (0, 1) else None)
-        for lo, hi in LATE_RUNS:
-            add_bf_run(0, lo, hi)
-        add_bf_run(1, EARLY, EARLY + 1)
+            quantise_w2(b, 0)
+        add_bf(0, 1, "bf1_0")
+        add_bf(1, 1, "bf0_0")
 
         def round_half_on_gpsimd(b, e):
-            nc.gpsimd.tensor_scalar(
-                experts_of(bf_runs, b, e, e + 1)[:, 0], w2_raw[(b, e)].rearrange("p j n -> p n j"), 1.0, 0.0, MULT, ADD
-            )
+            nc.gpsimd.tensor_scalar(bf_of(b, e), w2_raw[(b, e)].rearrange("p j n -> p n j"), 1.0, 0.0, MULT, ADD)
 
-        for e in range(1, EARLY):
-            for b in range(2):
-                if e in EARLY_ON_SCALAR:
-                    round_half(b, e, nc.scalar.copy)
-                else:
+        for e in range(HEAD, EARLY - 1):
+            if e not in EARLY_ON_SCALAR:
+                for b in range(2):
                     round_half_on_gpsimd(b, e)
+        for b in range(2):
+            round_half(b, 3, nc.scalar.copy)
+        early_hs = sbuf([P, 2 * GROUP_SLOTS * 4], BF16, "early_hs", "w2_whole3")
+        for g in range(2):
+            interleave(g, early_hs[:].bitcast(U32)[:, 2 * GATHER_EDGES[g] : 2 * GATHER_EDGES[g + 1]])
+            hs_bf[g] = early_hs[:, g * GROUP_SLOTS * 4 : (g + 1) * GROUP_SLOTS * 4]
+        for g in range(2, GROUPS):
+            add_picked(g, "picked%d" % (g - 2))
+            for u in range(2):
+                gather(u, g)
+        for b in range(2):
+            round_half(b, 6, nc.scalar.copy)
+        hs_bf[2] = sbuf([P, GROUP_SLOTS * 4], BF16, "late_hs2", "w2_whole6")[:]
+        interleave(2, hs_bf[2].bitcast(U32))
+        add_bf(1, 9)
+        for e in (9, 10):
+            for b in range(2):
+                round_half(b, e, nc.scalar.copy)
+        hs_bf[3] = sbuf([P, GROUP_SLOTS * 4], BF16, "late_hs3")[:]
 
-        early_hs = sbuf([P, 2 * GROUP_SLOTS * 4], BF16, "early_hs", "w2_whole%d" % EARLY_ON_SCALAR[-1])
-        for g in range(GROUPS):
-            if g < 2:
-                hs_bf[g] = early_hs[:, g * GROUP_SLOTS * 4 : (g + 1) * GROUP_SLOTS * 4]
-            else:
-                hs_bf[g] = sbuf([P, GROUP_SLOTS * 4], BF16, "late_hs%d" % g, "picked%d" % (g - 2))[:]
-            interleave(g)
-        for e in range(EARLY, E):
-            round_half(0, e, nc.scalar.copy)
-        round_half(1, EARLY, nc.scalar.copy)
-
-        add_code_run(0, 1, EARLY)
-        add_code_run(0, EARLY, E)
-        quantise_w2(0, 1, 5)
+        hs_codes = sbuf([P, S], U32, "hs_codes", "h_pairs1")
+        quantise_w2(0, 1, "h_pairs0")
         quantise_h(0)
+        nc.vector.tensor_copy(
+            out=hs_bf[3].bitcast(I32).rearrange("p (c i u) -> p c u i", i=4, u=2),
+            in_=picked[3][:].bitcast(I32).rearrange("p u (c i) -> p c u i", i=4),
+        )
         quantise_h(1)
-        quantise_w2(0, 5, EARLY)
+        quantise_w2(0, 5)
         quantise_h(2)
         quantise_h(3)
-        for lo, hi in LATE_RUNS:
-            quantise_w2(0, lo, hi)
-        y = [sbuf([P, S], F32, "y0", "w2_half0_%d" % SPLIT_LOAD), sbuf([P, S], F32, "y1")]
-        for g in range(GROUPS):
-            multiply(0, g, y[0])
-
-        add_code_run(1, 1, EARLY + 1, "bf0_%d" % LAST)
-        add_code_run(1, EARLY + 1, E)
-        quantise_w2(1, 1, 5)
-        quantise_w2(1, 5, EARLY)
-        quantise_w2(1, EARLY, EARLY + 1)
-        add_bf_run(1, EARLY + 1, SPLIT_LOAD, "codes0_%d" % EARLY)
-        add_bf_run(1, SPLIT_LOAD, E)
         for e in range(EARLY + 1, E):
+            round_half(0, e, nc.scalar.copy)
+        quantise_w2(0, 9)
+        quantise_w2(0, 13)
+        quantise_w2(0, LAST)
+        y = [sbuf([P, S], F32, "y0", "w2_half0_%d" % SPLIT_LOAD)]
+        for i in range(len(BANK_RUNS[0])):
+            multiply(0, i)
+
+        quantise_w2(1, 1, "bf0_%d" % LAST)
+        quantise_w2(1, 9, "bf0_13")
+        add_bf(1, 11, "codes0_%d" % LAST)
+        add_bf(1, 15)
+        y.append(sbuf([P, S], F32, "y1", "plane0_%d" % LAST))
+        for e in range(11, E):
             round_half(1, e, nc.scalar.copy)
-        quantise_w2(1, EARLY + 1, SPLIT_LOAD)
-        quantise_w2(1, SPLIT_LOAD, E)
-        for g in range(GROUPS):
-            multiply(1, g, y[1])
+        quantise_w2(1, 11)
+        quantise_w2(1, 15)
+        for i in range(4):
+            multiply(1, i)
 
         pieces = [(b, sum(widths[:i]), sum(widths[: i + 1])) for b, widths in enumerate(PIECE_WIDTHS) for i in range(len(widths))]
         terms = {}
-        turned = [sbuf([P, T // 2], F32, "turned%d" % i, "w2_whole%d" % i) for i in range(TURNED)]
+        turned = [sbuf([P, T // 2], F32, "turned%d" % i, ("w2_whole6", "w2_whole7")[i]) for i in range(TURNED)]
         res = {}
-        term_tags = {(1, 0): "w2_half1_14", (1, 1): "w2_half1_15"}
+        term_tags = {(0, 0): "w2_whole0", (0, 1): "w2_whole1", (1, 0): "w2_half1_14", (1, 1): "w2_half1_15", (2, 0): "w2_whole3", (2, 1): "w2_whole4"}
 
         def product(i, r):
             b, lo, hi = pieces[i]
@@ -331,11 +337,11 @@ def tile_moe_sup_lin_gelu_kernel(
             if i % 2 == 1:
                 turn_back(i - 1)
                 turn_back(i)
-        late_res = sbuf([P, T // 2], F32, "late_res", "w2_whole0")
-        last_res = sbuf([P, T // 2], F32, "last_res", "w2_whole1")
+        late_res = sbuf([P, T // 2], F32, "late_res", "w2_whole6")
+        last_res = sbuf([P, T // 2], F32, "last_res", "w2_whole7")
         for i in range(TURNED, len(pieces)):
             product(i, 0)
+            product(i, 1)
             if i > TURNED:
                 add_on_vector(i - 1)
-            product(i, 1)
         add_on_vector(len(pieces) - 1)

@@ -29,7 +29,7 @@ GATHER_EDGES = (0, 384, 1024, 1536, 2048)
 HEAD = 1
 EARLY = 10
 EARLY_ON_SCALAR = (3, 6)
-SPLIT_LOAD = 14
+SPLIT_LOAD = 12
 LAST = E - 1
 RUNS = (
     ((0, 1), (1, 5), (5, 9), (9, 13), (13, 15), (15, 16)),
@@ -112,7 +112,8 @@ def tile_moe_sup_lin_gelu_kernel(
         for b in range(2):
             for e in range(SPLIT_LOAD, E):
                 nc.sync.dma_start(out=w2_raw[(b, e)], in_=w2_rows[e][:, :, b * P : (b + 1) * P])
-            nc.sync.dma_start(out=gates[b][:], in_=gate_rows[:, :, b * T // 2 : (b + 1) * T // 2])
+                if e == LAST - 2 * b:
+                    nc.sync.dma_start(out=gates[b][:], in_=gate_rows[:, :, b * T // 2 : (b + 1) * T // 2])
 
         def round_w1(a, lo, hi):
             nc.vector.tensor_copy(
@@ -263,7 +264,7 @@ def tile_moe_sup_lin_gelu_kernel(
         quantise_w2(0, 9)
         quantise_w2(0, 13)
         quantise_w2(0, LAST)
-        y = [sbuf([P, S], F32, "y0", "w2_half0_%d" % SPLIT_LOAD)]
+        y = [sbuf([P, S], F32, "y0", "w2_half0_14")]
         for i in range(len(BANK_RUNS[0])):
             multiply(0, i)
 

@@ -20,7 +20,7 @@ GELU = mybir.ActivationFunctionType.Gelu_apprx_tanh
 
 P = 128
 BANKS = 8
-BANK_TOKENS = 256
+TOKEN_EDGES = ((0, 128, 384, 512, 768, 1024), (0, 256, 512, 768, 1024))
 GROUP = 4
 GROUP_SLOTS = GROUP * C
 GROUPS = E // GROUP
@@ -59,9 +59,9 @@ def tile_moe_sup_lin_gelu_kernel(
         slot_list = keep.tile([P, S // 16], U16, name="slot_list")
         pos_lists = [keep.tile([P, T // 16], U16, name="pos_list%d" % r) for r in range(2)]
         ident = sbuf([P, P], F32, "ident")
-        x_codes = [sbuf([P, BANK_TOKENS], U32, "x_first"), sbuf([P, T - BANK_TOKENS], U32, "x_rest")]
+        x_codes = [sbuf([P, T // 2], U32, "x_codes%d" % a) for a in range(2)]
         x_plane = sbuf([P, T], U8, "x_plane")
-        w1_raw = [sbuf([P, 4, H // 2], F32, "w1_raw%d" % a) for a in range(2)]
+        w1_raw = [sbuf([P, 2, H], F32, "w1_raw%d" % a) for a in range(2)]
         w1_bf = sbuf([P, 4, P, 4], BF16, "w1_bf")
         w1_codes = sbuf([P, 4, P], U32, "w1_codes")
         w1_plane = sbuf([P, 4, P], U8, "w1_plane")
@@ -85,21 +85,21 @@ def tile_moe_sup_lin_gelu_kernel(
 
         def add_bf(b, lo, tag=None):
             hi = run_of(b, lo)[1]
-            bf[(b, lo)] = sbuf([P, (hi - lo) * P * 4], BF16, "bf%d_%d" % (b, lo), tag)
+            bf[(b, lo)] = sbuf([P, (hi - lo) * P * 4], BF16, "bf%d_%d" % (b, lo), tag)[:]
 
         make_identity(nc, ident[:])
 
         w1_rows = w1.rearrange("(p j) c -> p j c", j=4)
         for a in range(2):
-            nc.sync.dma_start(out=w1_raw[a][:], in_=w1_rows[:, :, a * H // 2 : (a + 1) * H // 2])
+            nc.sync.dma_start(out=w1_raw[a][:], in_=w1_rows[:, 2 * a : 2 * a + 2, :])
         x_rows = x_words[0].rearrange("p t d -> p (t d)").bitcast(I32)
-        nc.sync.dma_start(out=x_codes[0][:].bitcast(I32), in_=x_rows[:, 0:BANK_TOKENS])
+        nc.sync.dma_start(out=x_codes[0][:].bitcast(I32), in_=x_rows[:, 0 : T // 2])
         nc.vector.memset(x_plane[:].bitcast(I32), 0)
         for q in range(4):
             nc.sync.dma_start(
                 out=x_plane[32 * q : 32 * q + 4, :].bitcast(I32), in_=x_scales[0, 4 * q : 4 * q + 4, :].bitcast(I32)
             )
-        nc.sync.dma_start(out=x_codes[1][:].bitcast(I32), in_=x_rows[:, BANK_TOKENS:T])
+        nc.sync.dma_start(out=x_codes[1][:].bitcast(I32), in_=x_rows[:, T // 2 : T])
         w2_rows = [w2[e].rearrange("(p j) n -> p j n", j=4) for e in range(E)]
         for e in range(SPLIT_LOAD):
             nc.sync.dma_start(out=w2_whole[e], in_=w2_rows[e])
@@ -117,7 +117,7 @@ def tile_moe_sup_lin_gelu_kernel(
 
         def round_w1(a, lo, hi):
             nc.vector.tensor_copy(
-                out=w1_bf[:].rearrange("p t m j -> p m j t")[:, a * P // 2 : (a + 1) * P // 2, :, lo:hi],
+                out=w1_bf[:].rearrange("p t m j -> p m j t")[:, :, 2 * a : 2 * a + 2, lo:hi],
                 in_=w1_raw[a][:].rearrange("p j (m t) -> p m j t", t=4)[:, :, :, lo:hi],
             )
 
@@ -134,16 +134,19 @@ def tile_moe_sup_lin_gelu_kernel(
         quantise_w1(1, 2)
         round_w1(1, 2, 4)
         quantise_w1(2, 4)
+        filled = 0
         for u in range(2):
-            for lo in range(0, T, BANK_TOKENS):
-                tokens = slice(lo, lo + BANK_TOKENS)
-                bank = psum_bank([P, 2, BANK_TOKENS], u * BANKS // 2 + lo // BANK_TOKENS)
+            for lo, hi in zip(TOKEN_EDGES[u], TOKEN_EDGES[u][1:]):
+                tokens = slice(lo, hi)
+                bank = psum_bank([P, 2, hi - lo], filled % BANKS)
+                filled = filled + 1
+                at = lo % (T // 2)
                 for d in range(2):
                     nc.tensor.matmul_mx(
                         out=bank[:, d, :],
                         lhsT=w1_codes[:, 2 * u + d, :].bitcast(FP8X4),
                         lhsT_scale=w1_plane[:, 2 * u + d, :],
-                        rhs=(x_codes[0][:] if lo == 0 else x_codes[1][:, lo - BANK_TOKENS : lo]).bitcast(FP8X4),
+                        rhs=x_codes[lo // (T // 2)][:, at : at + hi - lo].bitcast(FP8X4),
                         rhs_scale=x_plane[:, tokens],
                         start=True,
                         stop=True,
@@ -164,7 +167,7 @@ def tile_moe_sup_lin_gelu_kernel(
             hi = run_of(b, lo)[1]
             codes[(b, lo)] = sbuf([P, (hi - lo) * P], U32, "codes%d_%d" % (b, lo), tag)
             planes[(b, lo)] = sbuf([P, (hi - lo) * P], U8, "plane%d_%d" % (b, lo))
-            nc.vector.quantize_mx(out=codes[(b, lo)][:].bitcast(FP8X4), scales=planes[(b, lo)][:], in_=bf[(b, lo)][:])
+            nc.vector.quantize_mx(out=codes[(b, lo)][:].bitcast(FP8X4), scales=planes[(b, lo)][:], in_=bf[(b, lo)])
 
         def gather(u, g):
             nc.vector.tensor_copy(
@@ -211,23 +214,27 @@ def tile_moe_sup_lin_gelu_kernel(
                 gather(u, g)
 
         for lo, hi in RUNS[0]:
-            if lo != 1:
+            if lo not in (1, 5):
                 add_bf(0, lo)
         add_bf(1, 0)
         for b in range(2):
             round_half(b, 0, nc.vector.tensor_copy)
         for b in range(2):
             quantise_w2(b, 0)
-        add_bf(0, 1, "bf1_0")
-        add_bf(1, 1, "bf0_0")
-
-        def round_half_on_gpsimd(b, e):
-            nc.gpsimd.tensor_scalar(bf_of(b, e), w2_raw[(b, e)].rearrange("p j n -> p n j"), 1.0, 0.0, MULT, ADD)
-
+        early_bf = sbuf([P, 2 * 8 * P * 4], BF16, "early_bf", "bf1_0")
+        bf[(0, 1)] = early_bf[:, 0 : 4 * P * 4]
+        bf[(0, 5)] = early_bf[:, 4 * P * 4 : 8 * P * 4]
+        bf[(1, 1)] = early_bf[:, 8 * P * 4 : 16 * P * 4]
         for e in range(HEAD, EARLY - 1):
             if e not in EARLY_ON_SCALAR:
-                for b in range(2):
-                    round_half_on_gpsimd(b, e)
+                nc.gpsimd.tensor_scalar(
+                    early_bf[:].rearrange("p (b e n j) -> p b e n j", b=2, n=P, j=4)[:, :, e - 1],
+                    w2_whole[e].rearrange("p j (b n) -> p b n j", b=2),
+                    1.0,
+                    0.0,
+                    MULT,
+                    ADD,
+                )
         for b in range(2):
             round_half(b, 3, nc.scalar.copy)
         early_hs = sbuf([P, 2 * GROUP_SLOTS * 4], BF16, "early_hs", "w2_whole3")

@@ -20,7 +20,7 @@ GELU = mybir.ActivationFunctionType.Gelu_apprx_tanh
 
 P = 128
 BANKS = 8
-TOKEN_EDGES = ((0, 128, 384, 512, 768, 1024), (0, 256, 512, 768, 1024))
+TOKEN_EDGES = ((0, 128, 256, 512, 768, 1024), (0, 256, 512, 768, 1024))
 GROUP = 4
 GROUP_SLOTS = GROUP * C
 GROUPS = E // GROUP
@@ -60,7 +60,7 @@ def tile_moe_sup_lin_gelu_kernel(
         pos_lists = [keep.tile([P, T // 16], U16, name="pos_list%d" % r) for r in range(2)]
         ident = sbuf([P, P], F32, "ident")
         x_codes = [sbuf([P, T // 2], U32, "x_codes%d" % a) for a in range(2)]
-        x_plane = sbuf([P, T], U8, "x_plane")
+        x_plane = sbuf([P, T // 4], U8, "x_plane")
         w1_raw = [sbuf([P, 2, H], F32, "w1_raw%d" % a) for a in range(2)]
         w1_bf = sbuf([P, 4, P, 4], BF16, "w1_bf")
         w1_codes = sbuf([P, 4, P], U32, "w1_codes")
@@ -97,7 +97,8 @@ def tile_moe_sup_lin_gelu_kernel(
         nc.vector.memset(x_plane[:].bitcast(I32), 0)
         for q in range(4):
             nc.sync.dma_start(
-                out=x_plane[32 * q : 32 * q + 4, :].bitcast(I32), in_=x_scales[0, 4 * q : 4 * q + 4, :].bitcast(I32)
+                out=x_plane[32 * q : 32 * q + 16, :].bitcast(I32),
+                in_=x_scales[0, 4 * q : 4 * q + 4, :].bitcast(I32).rearrange("r (a c) -> a r c", a=4),
             )
         nc.sync.dma_start(out=x_codes[1][:].bitcast(I32), in_=x_rows[:, T // 2 : T])
         w2_rows = [w2[e].rearrange("(p j) n -> p j n", j=4) for e in range(E)]
@@ -105,14 +106,14 @@ def tile_moe_sup_lin_gelu_kernel(
             nc.sync.dma_start(out=w2_whole[e], in_=w2_rows[e])
             if e == 0:
                 nc.sync.dma_start(slot_list[:], offs)
-            if e == EARLY - 1:
-                nc.sync.dma_start(pos_lists[0][:], pos1)
-                nc.sync.dma_start(pos_lists[1][:], pos2)
         gate_rows = gate.rearrange("r p t -> p r t")
         for b in range(2):
             for e in range(SPLIT_LOAD, E):
                 nc.sync.dma_start(out=w2_raw[(b, e)], in_=w2_rows[e][:, :, b * P : (b + 1) * P])
-                if e == LAST - 2 * b:
+                if (b, e) == (0, LAST):
+                    nc.sync.dma_start(pos_lists[0][:], pos1)
+                    nc.sync.dma_start(pos_lists[1][:], pos2)
+                if e == LAST:
                     nc.sync.dma_start(out=gates[b][:], in_=gate_rows[:, :, b * T // 2 : (b + 1) * T // 2])
 
         def round_w1(a, lo, hi):
@@ -147,7 +148,7 @@ def tile_moe_sup_lin_gelu_kernel(
                         lhsT=w1_codes[:, 2 * u + d, :].bitcast(FP8X4),
                         lhsT_scale=w1_plane[:, 2 * u + d, :],
                         rhs=x_codes[lo // (T // 2)][:, at : at + hi - lo].bitcast(FP8X4),
-                        rhs_scale=x_plane[:, tokens],
+                        rhs_scale=x_plane[4 * (lo // 256) : P, lo % 256 : lo % 256 + hi - lo],
                         start=True,
                         stop=True,
                     )
@@ -275,23 +276,23 @@ def tile_moe_sup_lin_gelu_kernel(
         for i in range(len(BANK_RUNS[0])):
             multiply(0, i)
 
-        quantise_w2(1, 1, "bf0_%d" % LAST)
+        quantise_w2(1, 1, "w2_half0_%d" % LAST)
         quantise_w2(1, 9, "bf0_13")
         add_bf(1, 11, "codes0_%d" % LAST)
         add_bf(1, 15)
-        y.append(sbuf([P, S], F32, "y1", "plane0_%d" % LAST))
         for e in range(11, E):
             round_half(1, e, nc.scalar.copy)
         quantise_w2(1, 11)
         quantise_w2(1, 15)
+        y.append(sbuf([P, S], F32, "y1", "w2_half1_14"))
         for i in range(4):
             multiply(1, i)
 
         pieces = [(b, sum(widths[:i]), sum(widths[: i + 1])) for b, widths in enumerate(PIECE_WIDTHS) for i in range(len(widths))]
         terms = {}
-        turned = [sbuf([P, T // 2], F32, "turned%d" % i, ("w2_whole6", "w2_whole7")[i]) for i in range(TURNED)]
+        turned = [sbuf([P, T // 2], F32, "turned%d" % i, ("codes1_15", "w2_whole7")[i]) for i in range(TURNED)]
         res = {}
-        term_tags = {(0, 0): "w2_whole0", (0, 1): "w2_whole1", (1, 0): "w2_half1_14", (1, 1): "w2_half1_15", (2, 0): "w2_whole3", (2, 1): "w2_whole4"}
+        term_tags = {(0, 0): "w2_whole0", (0, 1): "w2_whole1", (1, 0): "w2_half1_15", (1, 1): "bf1_15", (2, 0): "w2_whole3", (2, 1): "w2_whole4"}
 
         def product(i, r):
             b, lo, hi = pieces[i]
@@ -345,7 +346,7 @@ def tile_moe_sup_lin_gelu_kernel(
             if i % 2 == 1:
                 turn_back(i - 1)
                 turn_back(i)
-        late_res = sbuf([P, T // 2], F32, "late_res", "w2_whole6")
+        late_res = sbuf([P, T // 2], F32, "late_res", "codes1_15")
         last_res = sbuf([P, T // 2], F32, "last_res", "w2_whole7")
         for i in range(TURNED, len(pieces)):
             product(i, 0)

@@ -16,6 +16,7 @@ U8 = mybir.dt.uint8
 FP8X4 = mybir.dt.float8_e4m3fn_x4
 MULT = mybir.AluOpType.mult
 ADD = mybir.AluOpType.add
+COPY = mybir.ActivationFunctionType.Copy
 GELU = mybir.ActivationFunctionType.Gelu_apprx_tanh
 
 P = 128
@@ -38,8 +39,7 @@ RUNS = (
 BANK_RUNS = (((0, 4), (4, 8), (8, 12), (12, 15), (15, 16)), ((0, 4), (4, 8), (8, 12), (12, 16)))
 Y_BANKS = ((0, 1, 2, 3, 7), (4, 5, 6, 7))
 
-PIECE_WIDTHS = ((512, 512), (512, 256, 256))
-TURNED = 2
+TURNED = ((0, 256), (256, 512))
 
 
 def tile_moe_sup_lin_gelu_kernel(
@@ -288,69 +288,80 @@ def tile_moe_sup_lin_gelu_kernel(
         for i in range(4):
             multiply(1, i)
 
-        pieces = [(b, sum(widths[:i]), sum(widths[: i + 1])) for b, widths in enumerate(PIECE_WIDTHS) for i in range(len(widths))]
-        terms = {}
-        turned = [sbuf([P, T // 2], F32, "turned%d" % i, ("codes1_15", "w2_whole7")[i]) for i in range(TURNED)]
-        res = {}
-        term_tags = {(0, 0): "w2_whole0", (0, 1): "w2_whole1", (1, 0): "w2_half1_15", (1, 1): "bf1_15", (2, 0): "w2_whole3", (2, 1): "w2_whole4"}
+        def picks(b, r, lo, hi):
+            return y[b][:].indirect(pos_lists[r][:, lo // 16 : hi // 16])
 
-        def product(i, r):
-            b, lo, hi = pieces[i]
-            terms[(i, r)] = sbuf([P, hi - lo], F32, "term%d_%d" % (i, r), term_tags.get((i, r)))
+        def product(term, b, r, lo, hi):
             at = lo % (T // 2)
-            nc.vector.tensor_tensor(
-                terms[(i, r)][:],
-                y[b][:].indirect(pos_lists[r][:, lo // 16 : hi // 16]),
-                gates[lo // (T // 2)][:, r, at : at + hi - lo],
-                MULT,
-            )
+            nc.vector.tensor_tensor(term, picks(b, r, lo, hi), gates[lo // (T // 2)][:, r, at : at + hi - lo], MULT)
 
-        def store(i):
-            b, lo, hi = pieces[i]
-            nc.sync.dma_start(out=out[b * P : (b + 1) * P, lo:hi], in_=res[i])
+        def add(res, first, second, b, lo, hi):
+            nc.vector.tensor_tensor(res, first, second, ADD)
+            nc.sync.dma_start(out=out[b * P : (b + 1) * P, lo:hi], in_=res)
 
-        def add_on_vector(i):
-            b, lo, hi = pieces[i]
-            res[i] = late_res[:, lo:hi] if i == TURNED else last_res[:, lo - T // 2 : hi - T // 2]
-            nc.vector.tensor_tensor(res[i], terms[(i, 0)][:], terms[(i, 1)][:], ADD)
-            store(i)
+        early_terms = [sbuf([P, T // 2], F32, "early_term%d" % r, "w2_whole%d" % r) for r in range(2)]
+        for r in range(2):
+            product(early_terms[r][:], 0, r, 0, T // 2)
+        mid_terms = sbuf([P, 2, T // 2], F32, "mid_terms", "w2_half1_15")
+        for r in range(2):
+            product(mid_terms[:, r], 0, r, T // 2, T)
+        early_res = sbuf([P, T // 2], F32, "early_res", "bf1_15")
+        add(early_res[:], early_terms[0][:], early_terms[1][:], 0, 0, T // 2)
+        mid_res = sbuf([P, T // 2], F32, "mid_res")
+        add(mid_res[:], mid_terms[:, 0], mid_terms[:, 1], 0, T // 2, T)
 
-        def add_turned(i):
-            width = pieces[i][2] - pieces[i][1]
-            bank = psum_bank([P, width], i)
-            for c in range(0, width, P):
+        blocks = TURNED[-1][1] // P
+        gate_cols = sbuf([P, 2, blocks], F32, "gate_cols")
+        for r in range(2):
+            bank = psum_bank([P, blocks, P], r)
+            for c in range(blocks):
+                nc.tensor.transpose(bank[:, c, :], gates[0][:, r, c * P : (c + 1) * P], ident[:])
+            nc.scalar.copy(out=gate_cols[:, r, :], in_=bank[:, :, 0])
+        fetched = {}
+        turned = {}
+        scaled = {}
+        for i, (lo, hi) in enumerate(TURNED):
+            turned[i] = psum_bank([P, 2, hi - lo], 2 + i)
+            for r in range(2):
+                fetched[(i, r)] = sbuf([P, hi - lo], F32, "fetched%d_%d" % (i, r))
+                nc.scalar.activation(fetched[(i, r)][:], picks(1, r, lo, hi), COPY)
+                for c in range(0, hi - lo, P):
+                    nc.tensor.transpose(turned[i][:, r, c : c + P], fetched[(i, r)][:, c : c + P], ident[:])
+        for i, (lo, hi) in enumerate(TURNED):
+            scaled[i] = sbuf([P, 2, hi - lo], F32, "scaled%d" % i)
+            for c in range(0, hi - lo, P):
+                block = (lo + c) // P
+                for r in range(2):
+                    nc.scalar.activation(
+                        out=scaled[i][:, r, c : c + P],
+                        in_=turned[i][:, r, c : c + P],
+                        func=COPY,
+                        scale=gate_cols[:, r, block : block + 1],
+                    )
+        for i, (lo, hi) in enumerate(TURNED):
+            bank = psum_bank([P, hi - lo], i)
+            for c in range(0, hi - lo, P):
                 for r in range(2):
                     nc.tensor.matmul(
                         bank[:, c : c + P],
-                        terms[(i, r)][:, c : c + P],
+                        scaled[i][:, r, c : c + P],
                         ident[:],
                         start=(r == 0),
                         stop=(r == 1),
                         is_transpose=True,
                     )
-            nc.scalar.copy(out=turned[i][:, 0:width], in_=bank[:])
+            res = sbuf([P, hi - lo], F32, "turned_res%d" % i)
+            nc.scalar.copy(out=res[:], in_=bank[:])
+            nc.sync.dma_start(out=out[P : 2 * P, lo:hi], in_=res[:])
 
-        def turn_back(i):
-            b, lo, hi = pieces[i]
-            bank = psum_bank([P, hi - lo], TURNED + i)
-            for c in range(0, hi - lo, P):
-                nc.tensor.transpose(bank[:, c : c + P], turned[i][:, c : c + P], ident[:])
-            res[i] = sbuf([P, hi - lo], F32, "res%d" % i)[:]
-            nc.scalar.copy(out=res[i], in_=bank[:])
-            store(i)
-
-        for i in range(TURNED):
-            product(i, 0)
-            product(i, 1)
-            add_turned(i)
-            if i % 2 == 1:
-                turn_back(i - 1)
-                turn_back(i)
-        late_res = sbuf([P, T // 2], F32, "late_res", "codes1_15")
-        last_res = sbuf([P, T // 2], F32, "last_res", "w2_whole7")
-        for i in range(TURNED, len(pieces)):
-            product(i, 0)
-            product(i, 1)
-            if i > TURNED:
-                add_on_vector(i - 1)
-        add_on_vector(len(pieces) - 1)
+        first = TURNED[-1][1]
+        middle = (first + T) // 2
+        late_first = sbuf([P, T - first], F32, "late_first", "w2_whole3")
+        product(late_first[:], 1, 0, first, T)
+        late = [(first, middle), (middle, T)]
+        late_second = [sbuf([P, hi - lo], F32, "late_second%d" % i) for i, (lo, hi) in enumerate(late)]
+        for i, (lo, hi) in enumerate(late):
+            product(late_second[i][:], 1, 1, lo, hi)
+        for i, (lo, hi) in enumerate(late):
+            res = sbuf([P, hi - lo], F32, "late_res%d" % i)
+            add(res[:], late_first[:, lo - first : hi - first], late_second[i][:], 1, lo, hi)

@@ -32,9 +32,10 @@ EARLY = 10
 EARLY_ON_SCALAR = (3, 6)
 SPLIT_LOAD = 12
 LAST = E - 1
+LATE_ON_VECTOR = (11, 12)
 RUNS = (
     ((0, 1), (1, 5), (5, 9), (9, 13), (13, 15), (15, 16)),
-    ((0, 1), (1, 9), (9, 11), (11, 15), (15, 16)),
+    ((0, 1), (1, 9), (9, 11), (11, 13), (13, 16)),
 )
 BANK_RUNS = (((0, 4), (4, 8), (8, 12), (12, 15), (15, 16)), ((0, 4), (4, 8), (8, 12), (12, 16)))
 Y_BANKS = ((0, 1, 2, 3, 7), (4, 5, 6, 7))
@@ -68,7 +69,7 @@ def tile_moe_sup_lin_gelu_kernel(
         h_pairs = [sbuf([P, T, 2], BF16, "h_pairs%d" % u) for u in range(2)]
         picked = {}
         hs_plane = sbuf([P, S], U8, "hs_plane")
-        gates = [sbuf([P, 2, T // 2], F32, "gates%d" % a) for a in range(2)]
+        gates = sbuf([P, 2, T], F32, "gates")
 
         w2_whole = [sbuf([P, 4, N], F32, "w2_whole%d" % e)[:] for e in range(SPLIT_LOAD)]
         w2_raw = {(b, e): w2_whole[e][:, :, b * P : (b + 1) * P] for b in range(2) for e in range(SPLIT_LOAD)}
@@ -114,7 +115,7 @@ def tile_moe_sup_lin_gelu_kernel(
                     nc.sync.dma_start(pos_lists[0][:], pos1)
                     nc.sync.dma_start(pos_lists[1][:], pos2)
                 if e == LAST:
-                    nc.sync.dma_start(out=gates[b][:], in_=gate_rows[:, :, b * T // 2 : (b + 1) * T // 2])
+                    nc.sync.dma_start(out=gates[:, :, b * T // 2 : (b + 1) * T // 2], in_=gate_rows[:, :, b * T // 2 : (b + 1) * T // 2])
 
         def round_w1(a, lo, hi):
             nc.vector.tensor_copy(
@@ -278,12 +279,12 @@ def tile_moe_sup_lin_gelu_kernel(
 
         quantise_w2(1, 1, "w2_half0_%d" % LAST)
         quantise_w2(1, 9, "bf0_13")
-        add_bf(1, 11, "codes0_%d" % LAST)
-        add_bf(1, 15)
+        add_bf(1, 11, "bf0_%d" % LAST)
+        add_bf(1, 13, "codes0_%d" % LAST)
         for e in range(11, E):
-            round_half(1, e, nc.scalar.copy)
+            round_half(1, e, nc.vector.tensor_copy if e in LATE_ON_VECTOR else nc.scalar.copy)
         quantise_w2(1, 11)
-        quantise_w2(1, 15)
+        quantise_w2(1, 13)
         y.append(sbuf([P, S], F32, "y1", "w2_half1_14"))
         for i in range(4):
             multiply(1, i)
@@ -292,30 +293,31 @@ def tile_moe_sup_lin_gelu_kernel(
             return y[b][:].indirect(pos_lists[r][:, lo // 16 : hi // 16])
 
         def product(term, b, r, lo, hi):
-            at = lo % (T // 2)
-            nc.vector.tensor_tensor(term, picks(b, r, lo, hi), gates[lo // (T // 2)][:, r, at : at + hi - lo], MULT)
+            nc.vector.tensor_tensor(term, picks(b, r, lo, hi), gates[:, r, lo:hi], MULT)
 
         def add(res, first, second, b, lo, hi):
             nc.vector.tensor_tensor(res, first, second, ADD)
             nc.sync.dma_start(out=out[b * P : (b + 1) * P, lo:hi], in_=res)
 
-        early_terms = [sbuf([P, T // 2], F32, "early_term%d" % r, "w2_whole%d" % r) for r in range(2)]
+        first_term = sbuf([P, T // 2], F32, "first_term")
+        held_terms = sbuf([P, 3, T // 2], F32, "held_terms", "codes0_%d" % LAST)
+        early_terms = [first_term[:], held_terms[:, 0]]
         for r in range(2):
-            product(early_terms[r][:], 0, r, 0, T // 2)
-        mid_terms = sbuf([P, 2, T // 2], F32, "mid_terms", "w2_half1_15")
+            product(early_terms[r], 0, r, 0, T // 2)
+        mid_terms = held_terms[:, 1:3]
         for r in range(2):
             product(mid_terms[:, r], 0, r, T // 2, T)
-        early_res = sbuf([P, T // 2], F32, "early_res", "bf1_15")
-        add(early_res[:], early_terms[0][:], early_terms[1][:], 0, 0, T // 2)
+        early_res = sbuf([P, T // 2], F32, "early_res")
+        add(early_res[:], early_terms[0], early_terms[1], 0, 0, T // 2)
         mid_res = sbuf([P, T // 2], F32, "mid_res")
         add(mid_res[:], mid_terms[:, 0], mid_terms[:, 1], 0, T // 2, T)
 
         blocks = TURNED[-1][1] // P
         gate_cols = sbuf([P, 2, blocks], F32, "gate_cols")
         for r in range(2):
-            bank = psum_bank([P, blocks, P], r)
+            bank = psum_bank([P, blocks, P], Y_BANKS[1][2 + r])
             for c in range(blocks):
-                nc.tensor.transpose(bank[:, c, :], gates[0][:, r, c * P : (c + 1) * P], ident[:])
+                nc.tensor.transpose(bank[:, c, :], gates[:, r, c * P : (c + 1) * P], ident[:])
             nc.scalar.copy(out=gate_cols[:, r, :], in_=bank[:, :, 0])
         fetched = {}
         turned = {}
@@ -352,7 +354,7 @@ def tile_moe_sup_lin_gelu_kernel(
                     )
             res = sbuf([P, hi - lo], F32, "turned_res%d" % i)
             nc.scalar.copy(out=res[:], in_=bank[:])
-            nc.sync.dma_start(out=out[P : 2 * P, lo:hi], in_=res[:])
+            nc.scalar.dma_start(out=out[P : 2 * P, lo:hi], in_=res[:])
 
         first = TURNED[-1][1]
         middle = (first + T) // 2

@@ -30,17 +30,17 @@ GATHER_EDGES = (0, 384, 1024, 1536, 2048)
 HEAD = 1
 EARLY = 10
 EARLY_ON_SCALAR = (3, 6)
-SPLIT_LOAD = 12
+SPLIT_LOAD = 13
 LAST = E - 1
-LATE_ON_VECTOR = (11, 12)
+LATE_ON_VECTOR = (11, 12, 13)
 RUNS = (
     ((0, 1), (1, 5), (5, 9), (9, 13), (13, 15), (15, 16)),
-    ((0, 1), (1, 9), (9, 11), (11, 13), (13, 16)),
+    ((0, 1), (1, 9), (9, 11), (11, 14), (14, 16)),
 )
 BANK_RUNS = (((0, 4), (4, 8), (8, 12), (12, 15), (15, 16)), ((0, 4), (4, 8), (8, 12), (12, 16)))
 Y_BANKS = ((0, 1, 2, 3, 7), (4, 5, 6, 7))
 
-TURNED = ((0, 256), (256, 512))
+TURNED = ((0, 256), (256, 512), (512, 640))
 
 
 def tile_moe_sup_lin_gelu_kernel(
@@ -107,15 +107,15 @@ def tile_moe_sup_lin_gelu_kernel(
             nc.sync.dma_start(out=w2_whole[e], in_=w2_rows[e])
             if e == 0:
                 nc.sync.dma_start(slot_list[:], offs)
-        gate_rows = gate.rearrange("r p t -> p r t")
         for b in range(2):
             for e in range(SPLIT_LOAD, E):
                 nc.sync.dma_start(out=w2_raw[(b, e)], in_=w2_rows[e][:, :, b * P : (b + 1) * P])
                 if (b, e) == (0, LAST):
                     nc.sync.dma_start(pos_lists[0][:], pos1)
                     nc.sync.dma_start(pos_lists[1][:], pos2)
-                if e == LAST:
-                    nc.sync.dma_start(out=gates[:, :, b * T // 2 : (b + 1) * T // 2], in_=gate_rows[:, :, b * T // 2 : (b + 1) * T // 2])
+                    nc.sync.dma_start(out=gates[:, 0, 0 : T // 2], in_=gate[0][:, 0 : T // 2])
+        nc.sync.dma_start(out=gates[:, 0, T // 2 : T], in_=gate[0][:, T // 2 : T])
+        nc.sync.dma_start(out=gates[:, 1, :], in_=gate[1])
 
         def round_w1(a, lo, hi):
             nc.vector.tensor_copy(
@@ -277,14 +277,14 @@ def tile_moe_sup_lin_gelu_kernel(
         for i in range(len(BANK_RUNS[0])):
             multiply(0, i)
 
-        quantise_w2(1, 1, "w2_half0_%d" % LAST)
-        quantise_w2(1, 9, "bf0_13")
         add_bf(1, 11, "bf0_%d" % LAST)
-        add_bf(1, 13, "codes0_%d" % LAST)
+        add_bf(1, 14, "codes0_%d" % LAST)
         for e in range(11, E):
             round_half(1, e, nc.vector.tensor_copy if e in LATE_ON_VECTOR else nc.scalar.copy)
+        quantise_w2(1, 1, "w2_half0_%d" % LAST)
+        quantise_w2(1, 9, "bf0_13")
         quantise_w2(1, 11)
-        quantise_w2(1, 13)
+        quantise_w2(1, 14)
         y.append(sbuf([P, S], F32, "y1", "w2_half1_14"))
         for i in range(4):
             multiply(1, i)
@@ -302,10 +302,9 @@ def tile_moe_sup_lin_gelu_kernel(
         first_term = sbuf([P, T // 2], F32, "first_term")
         held_terms = sbuf([P, 3, T // 2], F32, "held_terms", "codes0_%d" % LAST)
         early_terms = [first_term[:], held_terms[:, 0]]
-        for r in range(2):
-            product(early_terms[r], 0, r, 0, T // 2)
         mid_terms = held_terms[:, 1:3]
         for r in range(2):
+            product(early_terms[r], 0, r, 0, T // 2)
             product(mid_terms[:, r], 0, r, T // 2, T)
         early_res = sbuf([P, T // 2], F32, "early_res")
         add(early_res[:], early_terms[0], early_terms[1], 0, 0, T // 2)
@@ -313,12 +312,13 @@ def tile_moe_sup_lin_gelu_kernel(
         add(mid_res[:], mid_terms[:, 0], mid_terms[:, 1], 0, T // 2, T)
 
         blocks = TURNED[-1][1] // P
-        gate_cols = sbuf([P, 2, blocks], F32, "gate_cols")
-        for r in range(2):
-            bank = psum_bank([P, blocks, P], Y_BANKS[1][2 + r])
-            for c in range(blocks):
-                nc.tensor.transpose(bank[:, c, :], gates[:, r, c * P : (c + 1) * P], ident[:])
-            nc.scalar.copy(out=gate_cols[:, r, :], in_=bank[:, :, 0])
+        gate_cols = sbuf([P, blocks, 2], F32, "gate_cols")
+        for i, (lo, hi) in enumerate(TURNED):
+            bank = psum_bank([P, (hi - lo) // P, 2, P], Y_BANKS[1][1 + i])
+            for c in range(lo // P, hi // P):
+                for r in range(2):
+                    nc.tensor.transpose(bank[:, c - lo // P, r, :], gates[:, r, c * P : (c + 1) * P], ident[:])
+            nc.scalar.copy(out=gate_cols[:, lo // P : hi // P, :], in_=bank[:, :, :, 0])
         fetched = {}
         turned = {}
         scaled = {}
@@ -338,10 +338,10 @@ def tile_moe_sup_lin_gelu_kernel(
                         out=scaled[i][:, r, c : c + P],
                         in_=turned[i][:, r, c : c + P],
                         func=COPY,
-                        scale=gate_cols[:, r, block : block + 1],
+                        scale=gate_cols[:, block, r : r + 1],
                     )
         for i, (lo, hi) in enumerate(TURNED):
-            bank = psum_bank([P, hi - lo], i)
+            bank = psum_bank([P, hi - lo], (0, 1, 5)[i])
             for c in range(0, hi - lo, P):
                 for r in range(2):
                     nc.tensor.matmul(
@@ -357,7 +357,7 @@ def tile_moe_sup_lin_gelu_kernel(
             nc.scalar.dma_start(out=out[P : 2 * P, lo:hi], in_=res[:])
 
         first = TURNED[-1][1]
-        middle = (first + T) // 2
+        middle = T - P
         late_first = sbuf([P, T - first], F32, "late_first", "w2_whole3")
         product(late_first[:], 1, 0, first, T)
         late = [(first, middle), (middle, T)]

@@ -22,25 +22,26 @@ GELU = mybir.ActivationFunctionType.Gelu_apprx_tanh
 P = 128
 BANKS = 8
 TOKEN_EDGES = ((0, 128, 256, 512, 768, 1024), (0, 256, 512, 768, 1024))
-GROUP = 4
-GROUP_SLOTS = GROUP * C
-GROUPS = E // GROUP
+GROUP_SLOTS = 4 * C
+GROUPS = S // GROUP_SLOTS
 GATHER_EDGES = (0, 384, 1024, 1536, 2048)
 
-HEAD = 1
-EARLY = 10
+EARLY = range(1, 9)
 EARLY_ON_SCALAR = (3, 6)
+WHOLE_ON_SCALAR = (9, 10)
+LATE_ON_VECTOR = (11, 12)
+LATE_ON_SCALAR = (13, 14, 15)
 SPLIT_LOAD = 13
 LAST = E - 1
-LATE_ON_VECTOR = (11, 12, 13)
 RUNS = (
     ((0, 1), (1, 5), (5, 9), (9, 13), (13, 15), (15, 16)),
-    ((0, 1), (1, 9), (9, 11), (11, 14), (14, 16)),
+    ((0, 1), (1, 9), (9, 11), (11, 13), (13, 16)),
 )
 BANK_RUNS = (((0, 4), (4, 8), (8, 12), (12, 15), (15, 16)), ((0, 4), (4, 8), (8, 12), (12, 16)))
 Y_BANKS = ((0, 1, 2, 3, 7), (4, 5, 6, 7))
 
-TURNED = ((0, 256), (256, 512), (512, 640))
+TURNED = ((0, 256), (256, 512))
+LATE_PIECES = ((512, 768), (768, 896), (896, 1024))
 
 
 def tile_moe_sup_lin_gelu_kernel(
@@ -82,7 +83,7 @@ def tile_moe_sup_lin_gelu_kernel(
         planes = {}
 
         def run_of(b, e):
-            return [run for run in RUNS[b] if run[0] <= e < run[1]][0]
+            return [(lo, hi) for lo, hi in RUNS[b] if lo <= e < hi][0]
 
         def add_bf(b, lo, tag=None):
             hi = run_of(b, lo)[1]
@@ -193,12 +194,12 @@ def tile_moe_sup_lin_gelu_kernel(
             lo, hi = BANK_RUNS[b][i]
             bank = psum_bank([P, hi - lo, C], Y_BANKS[b][i])
             for e in range(lo, hi):
-                first = run_of(b, e)[0]
-                columns = slice((e - first) * P, (e - first + 1) * P)
+                run = run_of(b, e)[0]
+                columns = slice((e - run) * P, (e - run + 1) * P)
                 nc.tensor.matmul_mx(
                     out=bank[:, e - lo, :],
-                    lhsT=codes[(b, first)][:, columns].bitcast(FP8X4),
-                    lhsT_scale=planes[(b, first)][:, columns],
+                    lhsT=codes[(b, run)][:, columns].bitcast(FP8X4),
+                    lhsT_scale=planes[(b, run)][:, columns],
                     rhs=hs_codes[:, e * C : (e + 1) * C].bitcast(FP8X4),
                     rhs_scale=hs_plane[:, e * C : (e + 1) * C],
                     start=True,
@@ -216,7 +217,7 @@ def tile_moe_sup_lin_gelu_kernel(
                 gather(u, g)
 
         for lo, hi in RUNS[0]:
-            if lo not in (1, 5):
+            if lo not in EARLY:
                 add_bf(0, lo)
         add_bf(1, 0)
         for b in range(2):
@@ -227,10 +228,10 @@ def tile_moe_sup_lin_gelu_kernel(
         bf[(0, 1)] = early_bf[:, 0 : 4 * P * 4]
         bf[(0, 5)] = early_bf[:, 4 * P * 4 : 8 * P * 4]
         bf[(1, 1)] = early_bf[:, 8 * P * 4 : 16 * P * 4]
-        for e in range(HEAD, EARLY - 1):
+        for e in EARLY:
             if e not in EARLY_ON_SCALAR:
                 nc.gpsimd.tensor_scalar(
-                    early_bf[:].rearrange("p (b e n j) -> p b e n j", b=2, n=P, j=4)[:, :, e - 1],
+                    early_bf[:].rearrange("p (b e n j) -> p b e n j", b=2, n=P, j=4)[:, :, e - EARLY[0]],
                     w2_whole[e].rearrange("p j (b n) -> p b n j", b=2),
                     1.0,
                     0.0,
@@ -238,8 +239,8 @@ def tile_moe_sup_lin_gelu_kernel(
                     ADD,
                 )
         for b in range(2):
-            round_half(b, 3, nc.scalar.copy)
-        early_hs = sbuf([P, 2 * GROUP_SLOTS * 4], BF16, "early_hs", "w2_whole3")
+            round_half(b, EARLY_ON_SCALAR[0], nc.scalar.copy)
+        early_hs = sbuf([P, 2 * GROUP_SLOTS * 4], BF16, "early_hs", "w2_whole%d" % EARLY_ON_SCALAR[0])
         for g in range(2):
             interleave(g, early_hs[:].bitcast(U32)[:, 2 * GATHER_EDGES[g] : 2 * GATHER_EDGES[g + 1]])
             hs_bf[g] = early_hs[:, g * GROUP_SLOTS * 4 : (g + 1) * GROUP_SLOTS * 4]
@@ -248,11 +249,11 @@ def tile_moe_sup_lin_gelu_kernel(
             for u in range(2):
                 gather(u, g)
         for b in range(2):
-            round_half(b, 6, nc.scalar.copy)
-        hs_bf[2] = sbuf([P, GROUP_SLOTS * 4], BF16, "late_hs2", "w2_whole6")[:]
+            round_half(b, EARLY_ON_SCALAR[1], nc.scalar.copy)
+        hs_bf[2] = sbuf([P, GROUP_SLOTS * 4], BF16, "late_hs2", "w2_whole%d" % EARLY_ON_SCALAR[1])[:]
         interleave(2, hs_bf[2].bitcast(U32))
-        add_bf(1, 9)
-        for e in (9, 10):
+        add_bf(1, WHOLE_ON_SCALAR[0])
+        for e in WHOLE_ON_SCALAR:
             for b in range(2):
                 round_half(b, e, nc.scalar.copy)
         hs_bf[3] = sbuf([P, GROUP_SLOTS * 4], BF16, "late_hs3")[:]
@@ -268,25 +269,24 @@ def tile_moe_sup_lin_gelu_kernel(
         quantise_w2(0, 5)
         quantise_h(2)
         quantise_h(3)
-        for e in range(EARLY + 1, E):
+        for e in LATE_ON_VECTOR + LATE_ON_SCALAR:
             round_half(0, e, nc.scalar.copy)
-        quantise_w2(0, 9)
-        quantise_w2(0, 13)
-        quantise_w2(0, LAST)
-        y = [sbuf([P, S], F32, "y0", "w2_half0_14")]
+        for lo, hi in RUNS[0][3:]:
+            quantise_w2(0, lo)
+        y = [sbuf([P, S], F32, "y0", "w2_half0_%d" % (LAST - 1))]
         for i in range(len(BANK_RUNS[0])):
             multiply(0, i)
 
-        add_bf(1, 11, "bf0_%d" % LAST)
-        add_bf(1, 14, "codes0_%d" % LAST)
-        for e in range(11, E):
+        add_bf(1, LATE_ON_VECTOR[0], "bf0_%d" % LAST)
+        add_bf(1, LATE_ON_SCALAR[0], "codes0_%d" % LAST)
+        for e in LATE_ON_VECTOR + LATE_ON_SCALAR:
             round_half(1, e, nc.vector.tensor_copy if e in LATE_ON_VECTOR else nc.scalar.copy)
-        quantise_w2(1, 1, "w2_half0_%d" % LAST)
-        quantise_w2(1, 9, "bf0_13")
-        quantise_w2(1, 11)
-        quantise_w2(1, 14)
-        y.append(sbuf([P, S], F32, "y1", "w2_half1_14"))
-        for i in range(4):
+        quantise_w2(1, EARLY[0], "w2_half0_%d" % LAST)
+        quantise_w2(1, WHOLE_ON_SCALAR[0], "bf0_%d" % RUNS[0][-2][0])
+        quantise_w2(1, LATE_ON_VECTOR[0])
+        quantise_w2(1, LATE_ON_SCALAR[0])
+        y.append(sbuf([P, S], F32, "y1", "w2_half1_%d" % (LAST - 1)))
+        for i in range(len(BANK_RUNS[1])):
             multiply(1, i)
 
         def picks(b, r, lo, hi):
@@ -295,8 +295,8 @@ def tile_moe_sup_lin_gelu_kernel(
         def product(term, b, r, lo, hi):
             nc.vector.tensor_tensor(term, picks(b, r, lo, hi), gates[:, r, lo:hi], MULT)
 
-        def add(res, first, second, b, lo, hi):
-            nc.vector.tensor_tensor(res, first, second, ADD)
+        def add(res, term1, term2, b, lo, hi):
+            nc.vector.tensor_tensor(res, term1, term2, ADD)
             nc.sync.dma_start(out=out[b * P : (b + 1) * P, lo:hi], in_=res)
 
         first_term = sbuf([P, T // 2], F32, "first_term")
@@ -311,24 +311,22 @@ def tile_moe_sup_lin_gelu_kernel(
         mid_res = sbuf([P, T // 2], F32, "mid_res")
         add(mid_res[:], mid_terms[:, 0], mid_terms[:, 1], 0, T // 2, T)
 
-        blocks = TURNED[-1][1] // P
-        gate_cols = sbuf([P, blocks, 2], F32, "gate_cols")
+        gate_cols = sbuf([P, TURNED[-1][1] // P, 2], F32, "gate_cols")
         for i, (lo, hi) in enumerate(TURNED):
-            bank = psum_bank([P, (hi - lo) // P, 2, P], Y_BANKS[1][1 + i])
+            bank = psum_bank([P, (hi - lo) // P, 2, P], Y_BANKS[1][2 + i])
             for c in range(lo // P, hi // P):
                 for r in range(2):
                     nc.tensor.transpose(bank[:, c - lo // P, r, :], gates[:, r, c * P : (c + 1) * P], ident[:])
             nc.scalar.copy(out=gate_cols[:, lo // P : hi // P, :], in_=bank[:, :, :, 0])
-        fetched = {}
         turned = {}
         scaled = {}
         for i, (lo, hi) in enumerate(TURNED):
-            turned[i] = psum_bank([P, 2, hi - lo], 2 + i)
+            turned[i] = psum_bank([P, 2, hi - lo], len(TURNED) + i)
             for r in range(2):
-                fetched[(i, r)] = sbuf([P, hi - lo], F32, "fetched%d_%d" % (i, r))
-                nc.scalar.activation(fetched[(i, r)][:], picks(1, r, lo, hi), COPY)
+                fetched = sbuf([P, hi - lo], F32, "fetched%d_%d" % (i, r))
+                nc.scalar.activation(fetched[:], picks(1, r, lo, hi), COPY)
                 for c in range(0, hi - lo, P):
-                    nc.tensor.transpose(turned[i][:, r, c : c + P], fetched[(i, r)][:, c : c + P], ident[:])
+                    nc.tensor.transpose(turned[i][:, r, c : c + P], fetched[:, c : c + P], ident[:])
         for i, (lo, hi) in enumerate(TURNED):
             scaled[i] = sbuf([P, 2, hi - lo], F32, "scaled%d" % i)
             for c in range(0, hi - lo, P):
@@ -341,7 +339,7 @@ def tile_moe_sup_lin_gelu_kernel(
                         scale=gate_cols[:, block, r : r + 1],
                     )
         for i, (lo, hi) in enumerate(TURNED):
-            bank = psum_bank([P, hi - lo], (0, 1, 5)[i])
+            bank = psum_bank([P, hi - lo], i)
             for c in range(0, hi - lo, P):
                 for r in range(2):
                     nc.tensor.matmul(
@@ -356,14 +354,18 @@ def tile_moe_sup_lin_gelu_kernel(
             nc.scalar.copy(out=res[:], in_=bank[:])
             nc.scalar.dma_start(out=out[P : 2 * P, lo:hi], in_=res[:])
 
-        first = TURNED[-1][1]
-        middle = T - P
-        late_first = sbuf([P, T - first], F32, "late_first", "w2_whole3")
+        first = LATE_PIECES[0][0]
+        late_first = sbuf([P, T - first], F32, "late_first", "w2_whole%d" % EARLY_ON_SCALAR[0])
         product(late_first[:], 1, 0, first, T)
-        late = [(first, middle), (middle, T)]
-        late_second = [sbuf([P, hi - lo], F32, "late_second%d" % i) for i, (lo, hi) in enumerate(late)]
-        for i, (lo, hi) in enumerate(late):
-            product(late_second[i][:], 1, 1, lo, hi)
-        for i, (lo, hi) in enumerate(late):
+        late_second = [sbuf([P, hi - lo], F32, "late_second%d" % i) for i, (lo, hi) in enumerate(LATE_PIECES)]
+
+        def add_late(i):
+            lo, hi = LATE_PIECES[i]
             res = sbuf([P, hi - lo], F32, "late_res%d" % i)
             add(res[:], late_first[:, lo - first : hi - first], late_second[i][:], 1, lo, hi)
+
+        for i, (lo, hi) in enumerate(LATE_PIECES):
+            product(late_second[i][:], 1, 1, lo, hi)
+            if i > 0:
+                add_late(i - 1)
+        add_late(len(LATE_PIECES) - 1)

@@ -20,11 +20,14 @@ COPY = mybir.ActivationFunctionType.Copy
 GELU = mybir.ActivationFunctionType.Gelu_apprx_tanh
 
 P = 128
-BANKS = 8
-TOKEN_EDGES = ((0, 128, 256, 512, 768, 1024), (0, 256, 512, 768, 1024))
+FIRST_LAYER = (
+    ((0, 128, 0), (128, 256, 1), (256, 512, 2), (512, 768, 3), (768, 896, 4), (896, 1024, 5)),
+    ((512, 768, 6), (768, 1024, 7), (0, 256, 3), (256, 512, 4)),
+)
 GROUP_SLOTS = 4 * C
 GROUPS = S // GROUP_SLOTS
-GATHER_EDGES = (0, 384, 1024, 1536, 2048)
+GATHER_EDGES = (0, 384, 1152, 1536, 2048)
+H_CALLS = ((0, 512), (512, 1024), (1024, 1152), (1152, 1536), (1536, 2048))
 
 EARLY = range(1, 9)
 EARLY_ON_SCALAR = (3, 6)
@@ -137,12 +140,10 @@ def tile_moe_sup_lin_gelu_kernel(
         quantise_w1(1, 2)
         round_w1(1, 2, 4)
         quantise_w1(2, 4)
-        filled = 0
         for u in range(2):
-            for lo, hi in zip(TOKEN_EDGES[u], TOKEN_EDGES[u][1:]):
+            for lo, hi, number in FIRST_LAYER[u]:
                 tokens = slice(lo, hi)
-                bank = psum_bank([P, 2, hi - lo], filled % BANKS)
-                filled = filled + 1
+                bank = psum_bank([P, 2, hi - lo], number)
                 at = lo % (T // 2)
                 for d in range(2):
                     nc.tensor.matmul_mx(
@@ -187,7 +188,7 @@ def tile_moe_sup_lin_gelu_kernel(
             nc.scalar.copy(out=words.rearrange("p (s u) -> p s u", u=2), in_=picked[g][:].rearrange("p u s -> p s u"))
 
         def quantise_h(g):
-            slots = slice(g * GROUP_SLOTS, (g + 1) * GROUP_SLOTS)
+            slots = slice(H_CALLS[g][0], H_CALLS[g][1])
             nc.vector.quantize_mx(out=hs_codes[:, slots].bitcast(FP8X4), scales=hs_plane[:, slots], in_=hs_bf[g])
 
         def multiply(b, i):
@@ -240,35 +241,39 @@ def tile_moe_sup_lin_gelu_kernel(
                 )
         for b in range(2):
             round_half(b, EARLY_ON_SCALAR[0], nc.scalar.copy)
-        early_hs = sbuf([P, 2 * GROUP_SLOTS * 4], BF16, "early_hs", "w2_whole%d" % EARLY_ON_SCALAR[0])
+        early_hs = sbuf([P, GATHER_EDGES[2] * 4], BF16, "early_hs", "w2_whole%d" % EARLY_ON_SCALAR[0])
         for g in range(2):
             interleave(g, early_hs[:].bitcast(U32)[:, 2 * GATHER_EDGES[g] : 2 * GATHER_EDGES[g + 1]])
-            hs_bf[g] = early_hs[:, g * GROUP_SLOTS * 4 : (g + 1) * GROUP_SLOTS * 4]
+        for g in range(3):
+            hs_bf[g] = early_hs[:, H_CALLS[g][0] * 4 : H_CALLS[g][1] * 4]
+        late_picked = sbuf([P, 2 * (S - GATHER_EDGES[2])], U32, "late_picked", "picked0")
         for g in range(2, GROUPS):
-            add_picked(g, "picked%d" % (g - 2))
+            lo, hi = 2 * (GATHER_EDGES[g] - GATHER_EDGES[2]), 2 * (GATHER_EDGES[g + 1] - GATHER_EDGES[2])
+            picked[g] = late_picked[:, lo:hi].rearrange("p (u s) -> p u s", u=2)
             for u in range(2):
                 gather(u, g)
         for b in range(2):
             round_half(b, EARLY_ON_SCALAR[1], nc.scalar.copy)
-        hs_bf[2] = sbuf([P, GROUP_SLOTS * 4], BF16, "late_hs2", "w2_whole%d" % EARLY_ON_SCALAR[1])[:]
-        interleave(2, hs_bf[2].bitcast(U32))
+        hs_bf[3] = sbuf([P, 384 * 4], BF16, "late_hs2", "w2_whole%d" % EARLY_ON_SCALAR[1])[:]
+        interleave(2, hs_bf[3].bitcast(U32))
         add_bf(1, WHOLE_ON_SCALAR[0])
         for e in WHOLE_ON_SCALAR:
             for b in range(2):
                 round_half(b, e, nc.scalar.copy)
-        hs_bf[3] = sbuf([P, GROUP_SLOTS * 4], BF16, "late_hs3")[:]
+        hs_bf[4] = sbuf([P, GROUP_SLOTS * 4], BF16, "late_hs3")[:]
 
         hs_codes = sbuf([P, S], U32, "hs_codes", "h_pairs1")
         quantise_w2(0, 1, "h_pairs0")
         quantise_h(0)
         nc.vector.tensor_copy(
-            out=hs_bf[3].bitcast(I32).rearrange("p (c i u) -> p c u i", i=4, u=2),
+            out=hs_bf[4].bitcast(I32).rearrange("p (c i u) -> p c u i", i=4, u=2),
             in_=picked[3][:].bitcast(I32).rearrange("p u (c i) -> p c u i", i=4),
         )
         quantise_h(1)
         quantise_w2(0, 5)
         quantise_h(2)
         quantise_h(3)
+        quantise_h(4)
         for e in LATE_ON_VECTOR + LATE_ON_SCALAR:
             round_half(0, e, nc.scalar.copy)
         for lo, hi in RUNS[0][3:]:

@@ -231,13 +231,9 @@ def tile_moe_sup_lin_gelu_kernel(
         bf[(1, 1)] = early_bf[:, 8 * P * 4 : 16 * P * 4]
         for e in EARLY:
             if e not in EARLY_ON_SCALAR:
-                nc.gpsimd.tensor_scalar(
-                    early_bf[:].rearrange("p (b e n j) -> p b e n j", b=2, n=P, j=4)[:, :, e - EARLY[0]],
-                    w2_whole[e].rearrange("p j (b n) -> p b n j", b=2),
-                    1.0,
-                    0.0,
-                    MULT,
-                    ADD,
+                nc.gpsimd.tensor_copy(
+                    out=early_bf[:].rearrange("p (b e c i j) -> p e b c j i", b=2, c=P // 2, i=2, j=4)[:, e - EARLY[0]],
+                    in_=w2_whole[e].rearrange("p j (b c i) -> p b c j i", b=2, i=2),
                 )
         for b in range(2):
             round_half(b, EARLY_ON_SCALAR[0], nc.scalar.copy)
@@ -257,18 +253,16 @@ def tile_moe_sup_lin_gelu_kernel(
         hs_bf[3] = sbuf([P, 384 * 4], BF16, "late_hs2", "w2_whole%d" % EARLY_ON_SCALAR[1])[:]
         interleave(2, hs_bf[3].bitcast(U32))
         add_bf(1, WHOLE_ON_SCALAR[0])
-        for e in WHOLE_ON_SCALAR:
-            for b in range(2):
-                round_half(b, e, nc.scalar.copy)
-        hs_bf[4] = sbuf([P, GROUP_SLOTS * 4], BF16, "late_hs3")[:]
+        for b in range(2):
+            round_half(b, 9, nc.gpsimd.tensor_copy)
+        for b in range(2):
+            round_half(b, 10, nc.scalar.copy)
+        hs_bf[4] = sbuf([P, GROUP_SLOTS * 4], BF16, "late_hs3", "w2_whole10")[:]
+        interleave(3, hs_bf[4].bitcast(U32))
 
         hs_codes = sbuf([P, S], U32, "hs_codes", "h_pairs1")
         quantise_w2(0, 1, "h_pairs0")
         quantise_h(0)
-        nc.vector.tensor_copy(
-            out=hs_bf[4].bitcast(I32).rearrange("p (c i u) -> p c u i", i=4, u=2),
-            in_=picked[3][:].bitcast(I32).rearrange("p u (c i) -> p c u i", i=4),
-        )
         quantise_h(1)
         quantise_w2(0, 5)
         quantise_h(2)

@@ -26,8 +26,8 @@ FIRST_LAYER = (
 )
 GROUP_SLOTS = 4 * C
 GROUPS = S // GROUP_SLOTS
-GATHER_EDGES = (0, 384, 1152, 1536, 2048)
-H_CALLS = ((0, 512), (512, 1024), (1024, 1152), (1152, 1536), (1536, 2048))
+GATHER_EDGES = (0, 384, 1024, 1664, 2048)
+H_CALLS = ((0, 512), (512, 1024), (1024, 1536), (1536, 1664), (1664, 2048))
 
 EARLY = range(1, 9)
 EARLY_ON_SCALAR = (3, 6)
@@ -240,7 +240,7 @@ def tile_moe_sup_lin_gelu_kernel(
         early_hs = sbuf([P, GATHER_EDGES[2] * 4], BF16, "early_hs", "w2_whole%d" % EARLY_ON_SCALAR[0])
         for g in range(2):
             interleave(g, early_hs[:].bitcast(U32)[:, 2 * GATHER_EDGES[g] : 2 * GATHER_EDGES[g + 1]])
-        for g in range(3):
+        for g in range(2):
             hs_bf[g] = early_hs[:, H_CALLS[g][0] * 4 : H_CALLS[g][1] * 4]
         late_picked = sbuf([P, 2 * (S - GATHER_EDGES[2])], U32, "late_picked", "picked0")
         for g in range(2, GROUPS):
@@ -250,14 +250,16 @@ def tile_moe_sup_lin_gelu_kernel(
                 gather(u, g)
         for b in range(2):
             round_half(b, EARLY_ON_SCALAR[1], nc.scalar.copy)
-        hs_bf[3] = sbuf([P, 384 * 4], BF16, "late_hs2", "w2_whole%d" % EARLY_ON_SCALAR[1])[:]
-        interleave(2, hs_bf[3].bitcast(U32))
+        mid_hs = sbuf([P, (GATHER_EDGES[3] - GATHER_EDGES[2]) * 4], BF16, "late_hs2", "w2_whole%d" % EARLY_ON_SCALAR[1])
+        interleave(2, mid_hs[:].bitcast(U32))
+        for g in (2, 3):
+            hs_bf[g] = mid_hs[:, (H_CALLS[g][0] - GATHER_EDGES[2]) * 4 : (H_CALLS[g][1] - GATHER_EDGES[2]) * 4]
         add_bf(1, WHOLE_ON_SCALAR[0])
         for b in range(2):
             round_half(b, 9, nc.gpsimd.tensor_copy)
         for b in range(2):
             round_half(b, 10, nc.scalar.copy)
-        hs_bf[4] = sbuf([P, GROUP_SLOTS * 4], BF16, "late_hs3", "w2_whole10")[:]
+        hs_bf[4] = sbuf([P, (S - GATHER_EDGES[3]) * 4], BF16, "late_hs3", "w2_whole10")[:]
         interleave(3, hs_bf[4].bitcast(U32))
 
         hs_codes = sbuf([P, S], U32, "hs_codes", "h_pairs1")

from contextlib import ExitStack

import concourse.mybir as mybir
from concourse.masks import make_identity

K, T, E, C, H, N = 512, 1024, 16, 128, 512, 256
S = E * C
FLOPS = 2 * K * H * T + 2 * H * N * S

F32 = mybir.dt.float32
BF16 = mybir.dt.bfloat16
I32 = mybir.dt.int32
U32 = mybir.dt.uint32
U16 = mybir.dt.uint16
U8 = mybir.dt.uint8
FP8X4 = mybir.dt.float8_e4m3fn_x4
MULT = mybir.AluOpType.mult
ADD = mybir.AluOpType.add
COPY = mybir.ActivationFunctionType.Copy
GELU = mybir.ActivationFunctionType.Gelu_apprx_tanh

P = 128
FIRST_LAYER = (
    ((0, 128, 0), (128, 256, 1), (256, 512, 2), (512, 768, 3), (768, 896, 4), (896, 1024, 5)),
    ((512, 768, 6), (768, 1024, 7), (0, 256, 3), (256, 512, 4)),
)
GROUP_SLOTS = 4 * C
GROUPS = S // GROUP_SLOTS
GATHER_EDGES = (0, 384, 1024, 1664, 2048)
H_CALLS = ((0, 512), (512, 1024), (1024, 1536), (1536, 1664), (1664, 2048))

EARLY = range(1, 9)
EARLY_ON_SCALAR = (3, 6)
WHOLE_ON_SCALAR = (9, 10)
LATE_ON_VECTOR = (11, 12)
LATE_ON_SCALAR = (13, 14, 15)
SPLIT_LOAD = 13
LAST = E - 1
RUNS = (
    ((0, 1), (1, 5), (5, 9), (9, 13), (13, 15), (15, 16)),
    ((0, 1), (1, 9), (9, 11), (11, 13), (13, 16)),
)
BANK_RUNS = (((0, 4), (4, 8), (8, 12), (12, 15), (15, 16)), ((0, 4), (4, 8), (8, 12), (12, 16)))
Y_BANKS = ((0, 1, 2, 3, 7), (4, 5, 6, 7))

TURNED = ((0, 256), (256, 512))
LATE_PIECES = ((512, 768), (768, 896), (896, 1024))


def tile_moe_sup_lin_gelu_kernel(
    tc, x_words, x_scales, w1, w2, gate, offs, pos1, pos2, out
):
    nc = tc.nc
    with ExitStack() as ctx:
        keep = ctx.enter_context(tc.tile_pool(name="keep", bufs=1))
        psum = ctx.enter_context(tc.psum_pool(name="psum", bufs=1))

        def sbuf(shape, dtype, name, tag=None):
            return keep.tile(shape, dtype, name=name, tag=tag or name, align_bytes=64)

        def psum_bank(shape, number):
            return psum.tile(shape, F32, name="bank", tag="bank%d" % number)

        slot_list = keep.tile([P, S // 16], U16, name="slot_list")
        pos_lists = [keep.tile([P, T // 16], U16, name="pos_list%d" % r) for r in range(2)]
        ident = sbuf([P, P], F32, "ident")
        x_codes = [sbuf([P, T // 2], U32, "x_codes%d" % a) for a in range(2)]
        x_plane = sbuf([P, T // 4], U8, "x_plane")
        w1_raw = [sbuf([P, 2, H], F32, "w1_raw%d" % a) for a in range(2)]
        w1_bf = sbuf([P, 4, P, 4], BF16, "w1_bf")
        w1_codes = sbuf([P, 4, P], U32, "w1_codes")
        w1_plane = sbuf([P, 4, P], U8, "w1_plane")
        h_pairs = [sbuf([P, T, 2], BF16, "h_pairs%d" % u) for u in range(2)]
        picked = {}
        hs_plane = sbuf([P, S], U8, "hs_plane")
        gates = sbuf([P, 2, T], F32, "gates")

        w2_whole = [sbuf([P, 4, N], F32, "w2_whole%d" % e)[:] for e in range(SPLIT_LOAD)]
        w2_raw = {(b, e): w2_whole[e][:, :, b * P : (b + 1) * P] for b in range(2) for e in range(SPLIT_LOAD)}
        for e in range(SPLIT_LOAD, E):
            w2_raw[(0, e)] = sbuf([P, 4, P], F32, "w2_half0_%d" % e)[:]
            w2_raw[(1, e)] = sbuf([P, 4, P], F32, "w2_half1_%d" % e)[:]

        bf = {}
        codes = {}
        planes = {}

        def run_of(b, e):
            return [(lo, hi) for lo, hi in RUNS[b] if lo <= e < hi][0]

        def add_bf(b, lo, tag=None):
            hi = run_of(b, lo)[1]
            bf[(b, lo)] = sbuf([P, (hi - lo) * P * 4], BF16, "bf%d_%d" % (b, lo), tag)[:]

        make_identity(nc, ident[:])

        w1_rows = w1.rearrange("(p j) c -> p j c", j=4)
        for a in range(2):
            nc.sync.dma_start(out=w1_raw[a][:], in_=w1_rows[:, 2 * a : 2 * a + 2, :])
        x_rows = x_words[0].rearrange("p t d -> p (t d)").bitcast(I32)
        nc.sync.dma_start(out=x_codes[0][:].bitcast(I32), in_=x_rows[:, 0 : T // 2])
        nc.vector.memset(x_plane[:].bitcast(I32), 0)
        for q in range(4):
            nc.sync.dma_start(
                out=x_plane[32 * q : 32 * q + 16, :].bitcast(I32),
                in_=x_scales[0, 4 * q : 4 * q + 4, :].bitcast(I32).rearrange("r (a c) -> a r c", a=4),
            )
        nc.sync.dma_start(out=x_codes[1][:].bitcast(I32), in_=x_rows[:, T // 2 : T])
        w2_rows = [w2[e].rearrange("(p j) n -> p j n", j=4) for e in range(E)]
        for e in range(SPLIT_LOAD):
            nc.sync.dma_start(out=w2_whole[e], in_=w2_rows[e])
            if e == 0:
                nc.sync.dma_start(slot_list[:], offs)
        for b in range(2):
            for e in range(SPLIT_LOAD, E):
                nc.sync.dma_start(out=w2_raw[(b, e)], in_=w2_rows[e][:, :, b * P : (b + 1) * P])
                if (b, e) == (0, LAST):
                    nc.sync.dma_start(pos_lists[0][:], pos1)
                    nc.sync.dma_start(pos_lists[1][:], pos2)
                    nc.sync.dma_start(out=gates[:, 0, 0 : T // 2], in_=gate[0][:, 0 : T // 2])
        nc.sync.dma_start(out=gates[:, 0, T // 2 : T], in_=gate[0][:, T // 2 : T])
        nc.sync.dma_start(out=gates[:, 1, :], in_=gate[1])

        def round_w1(a, lo, hi):
            nc.vector.tensor_copy(
                out=w1_bf[:].rearrange("p t m j -> p m j t")[:, :, 2 * a : 2 * a + 2, lo:hi],
                in_=w1_raw[a][:].rearrange("p j (m t) -> p m j t", t=4)[:, :, :, lo:hi],
            )

        def quantise_w1(lo, hi):
            nc.vector.quantize_mx(
                out=w1_codes[:, lo:hi].rearrange("p t m -> p (t m)").bitcast(FP8X4),
                scales=w1_plane[:, lo:hi].rearrange("p t m -> p (t m)"),
                in_=w1_bf[:, lo:hi].rearrange("p t m j -> p (t m j)"),
            )

        round_w1(0, 0, 4)
        round_w1(1, 0, 2)
        quantise_w1(0, 1)
        quantise_w1(1, 2)
        round_w1(1, 2, 4)
        quantise_w1(2, 4)
        for u in range(2):
            for lo, hi, number in FIRST_LAYER[u]:
                tokens = slice(lo, hi)
                bank = psum_bank([P, 2, hi - lo], number)
                at = lo % (T // 2)
                for d in range(2):
                    nc.tensor.matmul_mx(
                        out=bank[:, d, :],
                        lhsT=w1_codes[:, 2 * u + d, :].bitcast(FP8X4),
                        lhsT_scale=w1_plane[:, 2 * u + d, :],
                        rhs=x_codes[lo // (T // 2)][:, at : at + hi - lo].bitcast(FP8X4),
                        rhs_scale=x_plane[4 * (lo // 256) : P, lo % 256 : lo % 256 + hi - lo],
                        start=True,
                        stop=True,
                    )
                nc.scalar.activation(out=h_pairs[u][:, tokens, :], in_=bank[:].rearrange("p d t -> p t d"), func=GELU)

        def bf_of(b, e):
            lo = run_of(b, e)[0]
            return bf[(b, lo)][:, (e - lo) * P * 4 : (e - lo + 1) * P * 4].rearrange("p (n j) -> p n j", j=4)

        def round_half(b, e, copy):
            copy(
                out=bf_of(b, e).rearrange("p (c i) j -> p c j i", i=2),
                in_=w2_raw[(b, e)].rearrange("p j (c i) -> p c j i", i=2),
            )

        def quantise_w2(b, lo, tag=None):
            hi = run_of(b, lo)[1]
            codes[(b, lo)] = sbuf([P, (hi - lo) * P], U32, "codes%d_%d" % (b, lo), tag)
            planes[(b, lo)] = sbuf([P, (hi - lo) * P], U8, "plane%d_%d" % (b, lo))
            nc.vector.quantize_mx(out=codes[(b, lo)][:].bitcast(FP8X4), scales=planes[(b, lo)][:], in_=bf[(b, lo)])

        def gather(u, g):
            nc.vector.tensor_copy(
                picked[g][:, u],
                h_pairs[u][:]
                .rearrange("p t d -> p (t d)")
                .bitcast(U32)
                .indirect(slot_list[:, GATHER_EDGES[g] // 16 : GATHER_EDGES[g + 1] // 16]),
            )

        hs_bf = {}

        def interleave(g, words):
            nc.scalar.copy(out=words.rearrange("p (s u) -> p s u", u=2), in_=picked[g][:].rearrange("p u s -> p s u"))

        def quantise_h(g):
            slots = slice(H_CALLS[g][0], H_CALLS[g][1])
            nc.vector.quantize_mx(out=hs_codes[:, slots].bitcast(FP8X4), scales=hs_plane[:, slots], in_=hs_bf[g])

        def multiply(b, i):
            lo, hi = BANK_RUNS[b][i]
            bank = psum_bank([P, hi - lo, C], Y_BANKS[b][i])
            for e in range(lo, hi):
                run = run_of(b, e)[0]
                columns = slice((e - run) * P, (e - run + 1) * P)
                nc.tensor.matmul_mx(
                    out=bank[:, e - lo, :],
                    lhsT=codes[(b, run)][:, columns].bitcast(FP8X4),
                    lhsT_scale=planes[(b, run)][:, columns],
                    rhs=hs_codes[:, e * C : (e + 1) * C].bitcast(FP8X4),
                    rhs_scale=hs_plane[:, e * C : (e + 1) * C],
                    start=True,
                    stop=True,
                )
            nc.scalar.copy(out=y[b][:, lo * C : hi * C], in_=bank[:].rearrange("p e c -> p (e c)"))

        def add_picked(g, tag=None):
            picked[g] = sbuf([P, 2, GATHER_EDGES[g + 1] - GATHER_EDGES[g]], U32, "picked%d" % g, tag)

        for g in range(2):
            add_picked(g)
        for u in range(2):
            for g in range(2):
                gather(u, g)

        for lo, hi in RUNS[0]:
            if lo not in EARLY:
                add_bf(0, lo)
        add_bf(1, 0)
        for b in range(2):
            round_half(b, 0, nc.vector.tensor_copy)
        for b in range(2):
            quantise_w2(b, 0)
        early_bf = sbuf([P, 2 * 8 * P * 4], BF16, "early_bf", "bf1_0")
        bf[(0, 1)] = early_bf[:, 0 : 4 * P * 4]
        bf[(0, 5)] = early_bf[:, 4 * P * 4 : 8 * P * 4]
        bf[(1, 1)] = early_bf[:, 8 * P * 4 : 16 * P * 4]
        for e in EARLY:
            if e not in EARLY_ON_SCALAR:
                nc.gpsimd.tensor_copy(
                    out=early_bf[:].rearrange("p (b e c i j) -> p e b c j i", b=2, c=P // 2, i=2, j=4)[:, e - EARLY[0]],
                    in_=w2_whole[e].rearrange("p j (b c i) -> p b c j i", b=2, i=2),
                )
        for b in range(2):
            round_half(b, EARLY_ON_SCALAR[0], nc.scalar.copy)
        early_hs = sbuf([P, GATHER_EDGES[2] * 4], BF16, "early_hs", "w2_whole%d" % EARLY_ON_SCALAR[0])
        for g in range(2):
            interleave(g, early_hs[:].bitcast(U32)[:, 2 * GATHER_EDGES[g] : 2 * GATHER_EDGES[g + 1]])
        for g in range(2):
            hs_bf[g] = early_hs[:, H_CALLS[g][0] * 4 : H_CALLS[g][1] * 4]
        late_picked = sbuf([P, 2 * (S - GATHER_EDGES[2])], U32, "late_picked", "picked0")
        for g in range(2, GROUPS):
            lo, hi = 2 * (GATHER_EDGES[g] - GATHER_EDGES[2]), 2 * (GATHER_EDGES[g + 1] - GATHER_EDGES[2])
            picked[g] = late_picked[:, lo:hi].rearrange("p (u s) -> p u s", u=2)
            for u in range(2):
                gather(u, g)
        for b in range(2):
            round_half(b, EARLY_ON_SCALAR[1], nc.scalar.copy)
        mid_hs = sbuf([P, (GATHER_EDGES[3] - GATHER_EDGES[2]) * 4], BF16, "late_hs2", "w2_whole%d" % EARLY_ON_SCALAR[1])
        interleave(2, mid_hs[:].bitcast(U32))
        for g in (2, 3):
            hs_bf[g] = mid_hs[:, (H_CALLS[g][0] - GATHER_EDGES[2]) * 4 : (H_CALLS[g][1] - GATHER_EDGES[2]) * 4]
        add_bf(1, WHOLE_ON_SCALAR[0])
        for b in range(2):
            round_half(b, 9, nc.gpsimd.tensor_copy)
        for b in range(2):
            round_half(b, 10, nc.scalar.copy)
        hs_bf[4] = sbuf([P, (S - GATHER_EDGES[3]) * 4], BF16, "late_hs3", "w2_whole10")[:]
        interleave(3, hs_bf[4].bitcast(U32))

        hs_codes = sbuf([P, S], U32, "hs_codes", "h_pairs1")
        quantise_w2(0, 1, "h_pairs0")
        quantise_h(0)
        quantise_h(1)
        quantise_w2(0, 5)
        quantise_h(2)
        quantise_h(3)
        quantise_h(4)
        for e in LATE_ON_VECTOR + LATE_ON_SCALAR:
            round_half(0, e, nc.scalar.copy)
        for lo, hi in RUNS[0][3:]:
            quantise_w2(0, lo)
        y = [sbuf([P, S], F32, "y0", "w2_half0_%d" % (LAST - 1))]
        for i in range(len(BANK_RUNS[0])):
            multiply(0, i)

        add_bf(1, LATE_ON_VECTOR[0], "bf0_%d" % LAST)
        add_bf(1, LATE_ON_SCALAR[0], "codes0_%d" % LAST)
        for e in LATE_ON_VECTOR + LATE_ON_SCALAR:
            round_half(1, e, nc.vector.tensor_copy if e in LATE_ON_VECTOR else nc.scalar.copy)
        quantise_w2(1, EARLY[0], "w2_half0_%d" % LAST)
        quantise_w2(1, WHOLE_ON_SCALAR[0], "bf0_%d" % RUNS[0][-2][0])
        quantise_w2(1, LATE_ON_VECTOR[0])
        quantise_w2(1, LATE_ON_SCALAR[0])
        y.append(sbuf([P, S], F32, "y1", "w2_half1_%d" % (LAST - 1)))
        for i in range(len(BANK_RUNS[1])):
            multiply(1, i)

        def picks(b, r, lo, hi):
            return y[b][:].indirect(pos_lists[r][:, lo // 16 : hi // 16])

        def product(term, b, r, lo, hi):
            nc.vector.tensor_tensor(term, picks(b, r, lo, hi), gates[:, r, lo:hi], MULT)

        def add(res, term1, term2, b, lo, hi):
            nc.vector.tensor_tensor(res, term1, term2, ADD)
            nc.sync.dma_start(out=out[b * P : (b + 1) * P, lo:hi], in_=res)

        first_term = sbuf([P, T // 2], F32, "first_term")
        held_terms = sbuf([P, 3, T // 2], F32, "held_terms", "codes0_%d" % LAST)
        early_terms = [first_term[:], held_terms[:, 0]]
        mid_terms = held_terms[:, 1:3]
        for r in range(2):
            product(early_terms[r], 0, r, 0, T // 2)
            product(mid_terms[:, r], 0, r, T // 2, T)
        early_res = sbuf([P, T // 2], F32, "early_res")
        add(early_res[:], early_terms[0], early_terms[1], 0, 0, T // 2)
        mid_res = sbuf([P, T // 2], F32, "mid_res")
        add(mid_res[:], mid_terms[:, 0], mid_terms[:, 1], 0, T // 2, T)

        gate_cols = sbuf([P, TURNED[-1][1] // P, 2], F32, "gate_cols")
        for i, (lo, hi) in enumerate(TURNED):
            bank = psum_bank([P, (hi - lo) // P, 2, P], Y_BANKS[1][2 + i])
            for c in range(lo // P, hi // P):
                for r in range(2):
                    nc.tensor.transpose(bank[:, c - lo // P, r, :], gates[:, r, c * P : (c + 1) * P], ident[:])
            nc.scalar.copy(out=gate_cols[:, lo // P : hi // P, :], in_=bank[:, :, :, 0])
        turned = {}
        scaled = {}
        for i, (lo, hi) in enumerate(TURNED):
            turned[i] = psum_bank([P, 2, hi - lo], len(TURNED) + i)
            for r in range(2):
                fetched = sbuf([P, hi - lo], F32, "fetched%d_%d" % (i, r))
                nc.scalar.activation(fetched[:], picks(1, r, lo, hi), COPY)
                for c in range(0, hi - lo, P):
                    nc.tensor.transpose(turned[i][:, r, c : c + P], fetched[:, c : c + P], ident[:])
        for i, (lo, hi) in enumerate(TURNED):
            scaled[i] = sbuf([P, 2, hi - lo], F32, "scaled%d" % i)
            for c in range(0, hi - lo, P):
                block = (lo + c) // P
                for r in range(2):
                    nc.scalar.activation(
                        out=scaled[i][:, r, c : c + P],
                        in_=turned[i][:, r, c : c + P],
                        func=COPY,
                        scale=gate_cols[:, block, r : r + 1],
                    )
        for i, (lo, hi) in enumerate(TURNED):
            bank = psum_bank([P, hi - lo], i)
            for c in range(0, hi - lo, P):
                for r in range(2):
                    nc.tensor.matmul(
                        bank[:, c : c + P],
                        scaled[i][:, r, c : c + P],
                        ident[:],
                        start=(r == 0),
                        stop=(r == 1),
                        is_transpose=True,
                    )
            res = sbuf([P, hi - lo], F32, "turned_res%d" % i)
            nc.scalar.copy(out=res[:], in_=bank[:])
            nc.scalar.dma_start(out=out[P : 2 * P, lo:hi], in_=res[:])

        first = LATE_PIECES[0][0]
        late_first = sbuf([P, T - first], F32, "late_first", "w2_whole%d" % EARLY_ON_SCALAR[0])
        product(late_first[:], 1, 0, first, T)
        late_second = [sbuf([P, hi - lo], F32, "late_second%d" % i) for i, (lo, hi) in enumerate(LATE_PIECES)]

        def add_late(i):
            lo, hi = LATE_PIECES[i]
            res = sbuf([P, hi - lo], F32, "late_res%d" % i)
            add(res[:], late_first[:, lo - first : hi - first], late_second[i][:], 1, lo, hi)

        for i, (lo, hi) in enumerate(LATE_PIECES):
            product(late_second[i][:], 1, 1, lo, hi)
            if i > 0:
                add_late(i - 1)
        add_late(len(LATE_PIECES) - 1)
